import numpy as np
import ml_dtypes


def mxq(x, axis, fmt="e4m3"):
    dtype, down = {"e4m3": (ml_dtypes.float8_e4m3fn, 7), "e5m2": (ml_dtypes.float8_e5m2, 14)}[fmt]
    v = np.moveaxis(np.asarray(x, np.float32).astype(ml_dtypes.bfloat16).astype(np.float64), axis, -1)
    blocks = v.reshape(v.shape[:-1] + (-1, 32))
    amax = np.abs(blocks).max(-1, keepdims=True)
    byte = np.maximum(np.where(amax > 0, np.frexp(amax)[1] - 1 + 127, 0) - down, 1)
    scale = np.exp2(byte - 127.0)
    codes = (blocks / scale).astype(np.float32).astype(dtype).astype(np.float64)
    return np.moveaxis((codes * scale).reshape(v.shape), -1, axis)


WIDE = False


def mx_kscale(k):
    if not WIDE:
        return np.ones(k)
    levels = np.array([10, -10, 5, -5, 0])
    if k % 512:
        return np.exp2(np.random.permutation(np.resize(levels, k // 32))).repeat(32)
    a = np.empty((k // 512, 16))
    for p in range(k // 512):
        a[p, :8] = np.random.permutation(np.resize(levels, 8))
        for g in range(8):
            far = levels[np.abs(levels - a[p, g]) >= 10]
            a[p, g + 8] = far[np.random.randint(len(far))]
    return np.exp2(a.ravel()).repeat(32)


def f64(x):
    return np.asarray(x).astype(np.float64)


def striped(idx):
    return np.tile(idx.reshape(-1, 16).T, (8, 1)).astype(np.uint16)


def unstriped(offs):
    return offs[:16].T.reshape(-1).astype(np.int64)


E2M1 = np.array([0.0, 0.5, 1.0, 1.5, 2.0, 3.0, 4.0, 6.0, -0.0, -0.5, -1.0, -1.5, -2.0, -3.0, -4.0, -6.0])


def pack_weight(w, fmt):
    k, n = w.shape
    w = f64(np.asarray(w, np.float32).astype(ml_dtypes.bfloat16)).reshape(k // 32, 32, n)
    amax = np.abs(w).max(1)
    if fmt == "e4m3":
        byte = np.frexp(amax)[1] - 1 + 127 - 7
    else:
        mant, ex = np.frexp(amax / 6.0)
        byte = np.where(mant > 0.5, ex, ex - 1) + 127
    byte = np.clip(np.where(amax > 0, byte, 1), 1, 254)
    scaled = (w * np.exp2(127.0 - byte)[:, None, :]).reshape(k, n).astype(np.float32)
    by_word = np.ascontiguousarray(scaled.reshape(k // 512, 128, 4, n).transpose(0, 1, 3, 2))
    if fmt == "e4m3":
        words = by_word.astype(ml_dtypes.float8_e4m3fn).view(np.uint8)
    else:
        c = by_word.astype(ml_dtypes.float4_e2m1fn).view(np.uint8) & 0xF
        words = (c[..., 0::2] | (c[..., 1::2] << 4)).reshape(k // 512, 128, 2 * n)
    return np.ascontiguousarray(words), np.ascontiguousarray(byte.astype(np.uint8).reshape(k // 512, 16, n))


def unpack_weight(words, scales, fmt):
    g, _, n = scales.shape
    words = np.ascontiguousarray(words).reshape(g, 128, n, -1)
    if fmt == "e4m3":
        vals = words.view(ml_dtypes.float8_e4m3fn).astype(np.float64)
    else:
        nib = np.empty((g, 128, n, 4), np.uint8)
        nib[..., 0::2] = words & 0xF
        nib[..., 1::2] = words >> 4
        vals = E2M1[nib]
    vals = vals * np.repeat(np.exp2(scales.astype(np.float64) - 127.0), 8, axis=1)[..., None]
    return vals.transpose(0, 1, 3, 2).reshape(g * 512, n)


def gelu(v):
    return 0.5 * v * (1.0 + np.tanh(np.sqrt(2.0 / np.pi) * (v + 0.044715 * v**3)))


K, H, N, T, S, T2 = 1024, 1024, 512, 2048, 1024, 2048

def setup_inputs():
    n = np.random.standard_normal
    s = mx_kscale(K)[:, None]
    u = mx_kscale(H)[:, None]
    tab_words, tab_scales = pack_weight(n((K, T)) * s, "e4m3")
    w4_words, w4_scales = pack_weight(1.5 * n((H, N)) / u / np.sqrt(H), "e2m1")
    return {
        "tab_words": tab_words, "tab_scales": tab_scales,
        "offs": striped(np.random.permutation(T)[:S]),
        "w1": (1.5 * n((K, H)) / s / np.sqrt(K)).astype(np.float32),
        "gain": (np.exp(0.3 * n(H)) * u[:, 0]).astype(np.float32),
        "w4_words": w4_words, "w4_scales": w4_scales,
        "wgo": np.exp(0.3 * n((128, S))).astype(np.float32),
        "offs2": striped(np.random.permutation(T2)[:S]),
    }

def reference(tab_words, tab_scales, offs, w1, gain, w4_words, w4_scales, wgo, offs2):
    v = unpack_weight(tab_words, tab_scales, "e4m3")[:, unstriped(offs)]
    w1q = mxq(f64(w1), 0, "e4m3")
    a = w1q.T @ v
    h = f64(gain)[:, None] * (np.log(1.0 + np.exp(a)) - np.log(2.0))
    hq = mxq(h, 0, "e4m3")
    w4 = unpack_weight(w4_words, w4_scales, "e2m1")
    y = w4.T @ hq
    out = np.zeros((N, T2))
    out[:, unstriped(offs2)] = np.tile(f64(wgo), (N // 128, 1)) * y
    return out

@@ -1,0 +1,261 @@
+import math
+from contextlib import ExitStack
+
+import concourse.mybir as mybir
+
+K, H, N, T, S, T2 = 1024, 1024, 512, 2048, 1024, 2048
+FLOPS = 2 * K * H * S + 2 * H * N * S
+
+F32 = mybir.dt.float32
+BF16 = mybir.dt.bfloat16
+I32 = mybir.dt.int32
+U32 = mybir.dt.uint32
+U16 = mybir.dt.uint16
+U8 = mybir.dt.uint8
+FP8X4 = mybir.dt.float8_e4m3fn_x4
+FP4X4 = mybir.dt.float4_e2m1fn_x4
+ALU = mybir.AluOpType
+ACT = mybir.ActivationFunctionType
+
+P = 128
+JC = 128
+NJC = S // JC
+EPS = 2.0**-60
+LN2 = math.log(2.0)
+GAIN_ON = "vvvvvvvv"
+SCATTER_TT = False
+
+
+def tile_list_bond_softplus_store_kernel(
+    tc, tab_words, tab_scales, offs, w1, gain, w4_words, w4_scales, wgo, offs2, out
+):
+    nc = tc.nc
+    with ExitStack() as ctx:
+        keep = ctx.enter_context(tc.tile_pool(name="keep", bufs=1))
+        psum = ctx.enter_context(tc.psum_pool(name="psum", bufs=1))
+
+        offs_t = keep.tile([P, S // 16], U16, name="offs_t")
+        offs2_t = keep.tile([P, S // 16], U16, name="offs2_t")
+        tab_sc = keep.tile([P, T], U8, name="tab_sc", align_bytes=64)
+        w4_sc = keep.tile([P, 2, N], U8, name="w4_sc", align_bytes=64)
+        tab_w = [keep.tile([P, T], I32, name=f"tab_w{a}", align_bytes=64) for a in range(2)]
+        w_raw = {(a, r): keep.tile([P, 4, 512], F32, name=f"w_raw{a}{r}") for a in range(2) for r in range(2)}
+        w_bf = {(a, r): keep.tile([P, 2048], BF16, name=f"w_bf{a}{r}", align_bytes=64) for a in range(2) for r in range(2)}
+        w_q = {(a, r): keep.tile([P, 512], U32, name=f"w_q{a}{r}", align_bytes=64) for a in range(2) for r in range(2)}
+        w_s = {(a, r): keep.tile([P, 512], U8, name=f"w_s{a}{r}", align_bytes=64) for a in range(2) for r in range(2)}
+        w4_t = keep.tile([P, 2, 2 * N], U8, name="w4_t", align_bytes=64)
+        wgo_t = keep.tile([P, S], F32, name="wgo_t")
+        gain_t = keep.tile([P, 2, 4], F32, name="gain_t")
+        gpat = keep.tile([P, 2, JC, 4], F32, name="gpat")
+        v_w = [[keep.tile([P, 512], U32, name=f"v_w{a}{b}", align_bytes=64) for b in range(2)] for a in range(2)]
+        v_s = [keep.tile([P, 512], U8, name=f"v_s{b}", align_bytes=64) for b in range(2)]
+        sig = [keep.tile([P, 2, 512], F32, name=f"sig{c}") for c in range(NJC)]
+        u_t = [keep.tile([P, 2, 512], F32, name=f"u{c}") for c in range(NJC)]
+        h_bf = [keep.tile([P, 1024], BF16, name=f"h_bf{c}", align_bytes=64) for c in range(NJC)]
+        h_q = [keep.tile([P, 2, JC], U32, name=f"h_q{c}", align_bytes=64) for c in range(NJC)]
+        h_s = [keep.tile([P, 2, JC], U8, name=f"h_s{c}", align_bytes=64) for c in range(NJC)]
+        yw = [keep.tile([P, 4, 256], F32, name=f"yw{b}") for b in range(4)]
+        win = [keep.tile([P, T2], F32, name=f"win{q}") for q in range(4)]
+        warm = keep.tile([P, 1], F32, name="warm")
+
+        nc.vector.memset(tab_sc[:].bitcast(I32), 0)
+        nc.vector.memset(w4_sc[:].rearrange("p a n -> p (a n)").bitcast(I32), 0)
+        nc.sync.dma_start(offs_t[:], offs)
+        for qd in range(4):
+            nc.sync.dma_start(
+                out=tab_sc[32 * qd : 32 * qd + 8, :].bitcast(I32),
+                in_=tab_scales[:, 4 * qd : 4 * qd + 4, :].bitcast(I32),
+            )
+        for qd in range(4):
+            nc.sync.dma_start(
+                out=w4_sc[32 * qd : 32 * qd + 4, :, :].bitcast(I32),
+                in_=w4_scales[:, 4 * qd : 4 * qd + 4, :].rearrange("a q n -> q a n").bitcast(I32),
+            )
+
+        def load_w(a, r):
+            nc.sync.dma_start(
+                out=w_raw[a, r][:],
+                in_=w1[512 * a : 512 * a + 512, 512 * r : 512 * r + 512].rearrange("(p j) c -> p j c", j=4),
+            )
+
+        def load_tab(a):
+            nc.sync.dma_start(out=tab_w[a][:], in_=tab_words[a].rearrange("p t i -> p (t i)").bitcast(I32))
+
+        load_tab(0)
+        load_w(0, 0)
+        load_tab(1)
+        load_w(1, 0)
+        load_w(0, 1)
+        load_w(1, 1)
+        nc.sync.dma_start(out=gain_t[:], in_=gain.rearrange("(a p t) -> p a t", a=2, t=4))
+        nc.sync.dma_start(
+            out=w4_t[:].bitcast(I32), in_=w4_words.rearrange("a p n -> p a n").bitcast(I32)
+        )
+        nc.sync.dma_start(out=wgo_t[:], in_=wgo)
+        nc.sync.dma_start(offs2_t[:], offs2)
+
+        for q in range(4):
+            nc.vector.memset(win[q][:].bitcast(I32), 0)
+
+        def gather_words(a, b):
+            nc.vector.tensor_copy(v_w[a][b][:], tab_w[a][:].bitcast(U32).indirect(offs_t[:, 32 * b : 32 * b + 32]))
+
+        def gather_scales(b):
+            nc.vector.tensor_copy(v_s[b][:], tab_sc[:].indirect(offs_t[:, 32 * b : 32 * b + 32]))
+
+        def cast_w(a, r, on_scalar):
+            dst = w_bf[a, r][:].rearrange("p (t m j) -> p m t j", t=4, j=4)
+            src = w_raw[a, r][:].rearrange("p j (m t) -> p m t j", t=4)
+            if on_scalar:
+                nc.scalar.activation(dst, src, ACT.Copy, scale=-1.0)
+            else:
+                nc.vector.tensor_scalar(dst, src, -1.0, None, ALU.mult)
+
+        def quant_w(a, r):
+            nc.vector.quantize_mx(out=w_q[a, r][:].bitcast(FP8X4), scales=w_s[a, r][:], in_=w_bf[a, r][:])
+
+        gather_words(0, 0)
+        cast_w(0, 0, True)
+        gather_scales(0)
+        quant_w(0, 0)
+        gather_words(1, 0)
+        cast_w(1, 0, True)
+        quant_w(1, 0)
+        cast_w(0, 1, False)
+        quant_w(0, 1)
+        cast_w(1, 1, False)
+        quant_w(1, 1)
+        gather_words(0, 1)
+        gather_scales(1)
+        gather_words(1, 1)
+        nc.vector.tensor_scalar(
+            gpat[:], gain_t[:].unsqueeze(2).to_broadcast([P, 2, JC, 4]), -1.0, None, ALU.mult
+        )
+
+        banks = {}
+
+        def first_product(r, c, slot):
+            bank = psum.tile([P, 4, JC], F32, name=f"a{r}{c}", tag=f"bank{slot}")
+            banks[r, c] = bank
+            b, cols = c // 4, slice(JC * (c % 4), JC * (c % 4 + 1))
+            for t in range(4):
+                for a in range(2):
+                    nc.tensor.matmul_mx(
+                        out=bank[:, t, :],
+                        lhsT=w_q[a, r][:, 128 * t : 128 * t + 128].bitcast(FP8X4),
+                        lhsT_scale=w_s[a, r][:, 128 * t : 128 * t + 128],
+                        rhs=v_w[a][b][:, cols].bitcast(FP8X4),
+                        rhs_scale=v_s[b][4 * a : 128, cols],
+                        start=(a == 0),
+                        stop=(a == 1),
+                    )
+
+        def sigmoid(r, c):
+            nc.scalar.activation(
+                sig[c][:, r, :].rearrange("p (j t) -> p j t", t=4),
+                banks[r, c][:].rearrange("p t j -> p j t"),
+                ACT.Sigmoid,
+            )
+
+        def log(c):
+            flat = sig[c][:].rearrange("p r x -> p (r x)")
+            nc.scalar.activation(flat, flat, ACT.Ln, bias=EPS, scale=2.0)
+
+        def guard(r, c):
+            nc.vector.scalar_tensor_tensor(
+                u_t[c][:, r, :].rearrange("p (j t) -> p j t", t=4),
+                banks[r, c][:].rearrange("p t j -> p j t"),
+                LN2,
+                sig[c][:, r, :].rearrange("p (j t) -> p j t", t=4),
+                ALU.add,
+                ALU.min,
+            )
+
+        def apply_gain(c):
+            eng = nc.gpsimd if GAIN_ON[c] == "g" else nc.vector
+            eng.tensor_tensor(
+                h_bf[c][:],
+                u_t[c][:].rearrange("p r x -> p (r x)"),
+                gpat[:].rearrange("p r j t -> p (r j t)"),
+                ALU.mult,
+            )
+
+        def quant_h(c):
+            nc.vector.quantize_mx(
+                out=h_q[c][:].rearrange("p r j -> p (r j)").bitcast(FP8X4),
+                scales=h_s[c][:].rearrange("p r j -> p (r j)"),
+                in_=h_bf[c][:],
+            )
+
+        def second_product(c, slot):
+            bank = psum.tile([P, 4, JC], F32, name=f"y{c}", tag=f"bank{slot}")
+            for q in range(4):
+                for r in range(2):
+                    nc.tensor.matmul_mx(
+                        out=bank[:, q, :],
+                        lhsT=w4_t[:, r, 256 * q : 256 * q + 256].bitcast(FP4X4),
+                        lhsT_scale=w4_sc[:, r, 128 * q : 128 * q + 128],
+                        rhs=h_q[c][:, r, :].bitcast(FP8X4),
+                        rhs_scale=h_s[c][:, r, :],
+                        start=(r == 0),
+                        stop=(r == 1),
+                    )
+            dst = yw[c // 2][:, :, JC * (c % 2) : JC * (c % 2 + 1)]
+            if SCATTER_TT:
+                nc.scalar.copy(dst, bank[:])
+            else:
+                nc.vector.tensor_tensor(
+                    dst, bank[:], wgo_t[:, JC * c : JC * (c + 1)].unsqueeze(1).to_broadcast([P, 4, JC]), ALU.mult
+                )
+
+        def scatter(b, q):
+            dst = win[q][:].indirect(offs2_t[:, 16 * b : 16 * b + 16])
+            if SCATTER_TT:
+                nc.vector.tensor_tensor(dst, yw[b][:, q, :], wgo_t[:, 256 * b : 256 * b + 256], ALU.mult)
+            else:
+                nc.vector.tensor_copy(dst, yw[b][:, q, :])
+
+        nc.vector.memset(warm[:], 0.0)
+        nc.scalar.activation(warm[:], warm[:], ACT.Sigmoid)
+
+        for r in range(2):
+            for c in range(4):
+                first_product(r, c, 2 * c + r)
+                sigmoid(r, c)
+        for c in range(4):
+            log(c)
+            guard(0, c)
+            guard(1, c)
+        for c in range(4):
+            apply_gain(c)
+            quant_h(c)
+        for c in range(4, 7):
+            for r in range(2):
+                first_product(r, c, 2 * (c - 4) + r)
+        second_product(0, 6)
+        second_product(1, 7)
+        for r in range(2):
+            first_product(r, 7, 6 + r)
+        for c in range(4, 8):
+            for r in range(2):
+                sigmoid(r, c)
+        for q in range(4):
+            scatter(0, q)
+        for c in range(4, 8):
+            log(c)
+            guard(0, c)
+            guard(1, c)
+            if c == 4:
+                second_product(2, 0)
+                second_product(3, 1)
+        for q in range(4):
+            scatter(1, q)
+        for c in range(4, 8):
+            apply_gain(c)
+            quant_h(c)
+            second_product(c, 2 + c % 4)
+        for q in range(4):
+            scatter(2, q)
+        for q in range(4):
+            scatter(3, q)
+            nc.sync.dma_start(out=out[128 * q : 128 * q + 128, :], in_=win[q][:])

@@ -22,8 +22,13 @@ JC = 128
 NJC = S // JC
 EPS = 2.0**-60
 LN2 = math.log(2.0)
-GAIN_ON = "vvvvvvvv"
-SCATTER_TT = False
+PLAN = [('G', 1), ('B', [(0, 0), (0, 1), (0, 2), (0, 3), (0, 4), (0, 5), (1, 0), (1, 1)], 'g'), ('Y', 0, 0, 0), ('Y', 0, 1, 0), ('Y', 0, 2, 0), ('Y', 0, 3, 0), ('S', 0, 0), ('S', 0, 1), ('S', 0, 2), ('S', 0, 3), ('B', [(1, 2), (1, 3), (0, 6), (0, 7), (1, 4), (1, 5), (1, 6), (1, 7)], 'g'), ('Y', 1, 0, 0), ('Y', 1, 1, 0), ('Y', 1, 2, 0), ('Y', 1, 3, 0), ('Y', 2, 0, 0), ('Y', 2, 1, 0), ('Y', 2, 2, 0), ('Y', 2, 3, 0), ('S', 1, 0), ('S', 1, 1), ('S', 1, 2), ('S', 1, 3), ('S', 2, 0), ('S', 2, 1), ('S', 2, 2), ('S', 2, 3)]
+GROUPS = [(0, 2), (2, 4), (4, 8)]
+CASTS = 'sssvssvv'
+GAIN_ON = 'gvvvvvgvvvggvvvv'
+TT = True
+GATHERS = [(0, 3), (3, 8)]
+TABFIRST = True
 
 
 def tile_list_bond_softplus_store_kernel(
@@ -39,105 +44,105 @@ def tile_list_bond_softplus_store_kernel(
         tab_sc = keep.tile([P, T], U8, name="tab_sc", align_bytes=64)
         w4_sc = keep.tile([P, 2, N], U8, name="w4_sc", align_bytes=64)
         tab_w = [keep.tile([P, T], I32, name=f"tab_w{a}", align_bytes=64) for a in range(2)]
-        w_raw = {(a, r): keep.tile([P, 4, 512], F32, name=f"w_raw{a}{r}") for a in range(2) for r in range(2)}
-        w_bf = {(a, r): keep.tile([P, 2048], BF16, name=f"w_bf{a}{r}", align_bytes=64) for a in range(2) for r in range(2)}
-        w_q = {(a, r): keep.tile([P, 512], U32, name=f"w_q{a}{r}", align_bytes=64) for a in range(2) for r in range(2)}
-        w_s = {(a, r): keep.tile([P, 512], U8, name=f"w_s{a}{r}", align_bytes=64) for a in range(2) for r in range(2)}
+        ar = [(a, r) for a in range(2) for r in range(2)]
+        w_raw = {(a, r, u): keep.tile([P, 4, 256], F32, name=f"w_raw{a}{r}{u}") for a, r in ar for u in range(2)}
+        w_bf = {k: keep.tile([P, 2048], BF16, name=f"w_bf{k[0]}{k[1]}", align_bytes=64) for k in ar}
+        w_q = {k: keep.tile([P, 512], U32, name=f"w_q{k[0]}{k[1]}", align_bytes=64) for k in ar}
+        w_s = {k: keep.tile([P, 512], U8, name=f"w_s{k[0]}{k[1]}", align_bytes=64) for k in ar}
         w4_t = keep.tile([P, 2, 2 * N], U8, name="w4_t", align_bytes=64)
         wgo_t = keep.tile([P, S], F32, name="wgo_t")
         gain_t = keep.tile([P, 2, 4], F32, name="gain_t")
-        gpat = keep.tile([P, 2, JC, 4], F32, name="gpat")
-        v_w = [[keep.tile([P, 512], U32, name=f"v_w{a}{b}", align_bytes=64) for b in range(2)] for a in range(2)]
-        v_s = [keep.tile([P, 512], U8, name=f"v_s{b}", align_bytes=64) for b in range(2)]
+        ngain = keep.tile([P, 2, 4], F32, name="ngain")
+        ng = len(GATHERS)
+        v_w = [[keep.tile([P, JC * (hi - lo)], U32, name=f"v_w{a}{lo}", align_bytes=64) for lo, hi in GATHERS] for a in range(2)]
+        v_s = [keep.tile([P, JC * (hi - lo)], U8, name=f"v_s{lo}", align_bytes=64) for lo, hi in GATHERS]
         sig = [keep.tile([P, 2, 512], F32, name=f"sig{c}") for c in range(NJC)]
-        u_t = [keep.tile([P, 2, 512], F32, name=f"u{c}") for c in range(NJC)]
-        h_bf = [keep.tile([P, 1024], BF16, name=f"h_bf{c}", align_bytes=64) for c in range(NJC)]
+        h_bf = [keep.tile([P, 2, 512], BF16, name=f"h_bf{c}", align_bytes=64) for c in range(NJC)]
         h_q = [keep.tile([P, 2, JC], U32, name=f"h_q{c}", align_bytes=64) for c in range(NJC)]
         h_s = [keep.tile([P, 2, JC], U8, name=f"h_s{c}", align_bytes=64) for c in range(NJC)]
-        yw = [keep.tile([P, 4, 256], F32, name=f"yw{b}") for b in range(4)]
+        y_sb = {(g, q): keep.tile([P, JC * (GROUPS[g][1] - GROUPS[g][0])], F32, name=f"y{g}{q}") for g in range(len(GROUPS)) for q in range(4)}
         win = [keep.tile([P, T2], F32, name=f"win{q}") for q in range(4)]
         warm = keep.tile([P, 1], F32, name="warm")
 
-        nc.vector.memset(tab_sc[:].bitcast(I32), 0)
-        nc.vector.memset(w4_sc[:].rearrange("p a n -> p (a n)").bitcast(I32), 0)
+        def load_w(a, r):
+            for u in range(2):
+                lo = 512 * r + 256 * u
+                nc.sync.dma_start(
+                    out=w_raw[a, r, u][:],
+                    in_=w1[512 * a : 512 * a + 512, lo : lo + 256].rearrange("(p j) c -> p j c", j=4),
+                )
+
+        def load_tab(a):
+            nc.sync.dma_start(out=tab_w[a][:], in_=tab_words[a].rearrange("p t i -> p (t i)").bitcast(I32))
+
+        nc.gpsimd.memset(tab_sc[:].bitcast(I32), 0)
+        nc.vector.memset(warm[:], 0.0)
+        nc.gpsimd.memset(w4_sc[:].rearrange("p a n -> p (a n)").bitcast(I32), 0)
+        for q in range(4):
+            nc.gpsimd.memset(win[q][:].bitcast(I32), 0)
+        load_tab(0)
         nc.sync.dma_start(offs_t[:], offs)
         for qd in range(4):
             nc.sync.dma_start(
                 out=tab_sc[32 * qd : 32 * qd + 8, :].bitcast(I32),
                 in_=tab_scales[:, 4 * qd : 4 * qd + 4, :].bitcast(I32),
             )
+        if TABFIRST:
+            load_tab(1)
+            load_w(0, 0)
+        else:
+            load_w(0, 0)
+            load_tab(1)
+        load_w(1, 0)
+        load_w(0, 1)
+        load_w(1, 1)
+        nc.sync.dma_start(out=gain_t[:], in_=gain.rearrange("(a p t) -> p a t", a=2, t=4))
         for qd in range(4):
             nc.sync.dma_start(
                 out=w4_sc[32 * qd : 32 * qd + 4, :, :].bitcast(I32),
                 in_=w4_scales[:, 4 * qd : 4 * qd + 4, :].rearrange("a q n -> q a n").bitcast(I32),
             )
-
-        def load_w(a, r):
-            nc.sync.dma_start(
-                out=w_raw[a, r][:],
-                in_=w1[512 * a : 512 * a + 512, 512 * r : 512 * r + 512].rearrange("(p j) c -> p j c", j=4),
-            )
-
-        def load_tab(a):
-            nc.sync.dma_start(out=tab_w[a][:], in_=tab_words[a].rearrange("p t i -> p (t i)").bitcast(I32))
-
-        load_tab(0)
-        load_w(0, 0)
-        load_tab(1)
-        load_w(1, 0)
-        load_w(0, 1)
-        load_w(1, 1)
-        nc.sync.dma_start(out=gain_t[:], in_=gain.rearrange("(a p t) -> p a t", a=2, t=4))
-        nc.sync.dma_start(
-            out=w4_t[:].bitcast(I32), in_=w4_words.rearrange("a p n -> p a n").bitcast(I32)
-        )
+        nc.sync.dma_start(out=w4_t[:].bitcast(I32), in_=w4_words.rearrange("a p n -> p a n").bitcast(I32))
         nc.sync.dma_start(out=wgo_t[:], in_=wgo)
         nc.sync.dma_start(offs2_t[:], offs2)
 
-        for q in range(4):
-            nc.vector.memset(win[q][:].bitcast(I32), 0)
+        def gather(g):
+            cols = slice(8 * GATHERS[g][0], 8 * GATHERS[g][1])
+            nc.vector.tensor_copy(v_w[0][g][:], tab_w[0][:].bitcast(U32).indirect(offs_t[:, cols]))
+            nc.vector.tensor_copy(v_s[g][:], tab_sc[:].indirect(offs_t[:, cols]))
+            nc.vector.tensor_copy(v_w[1][g][:], tab_w[1][:].bitcast(U32).indirect(offs_t[:, cols]))
 
-        def gather_words(a, b):
-            nc.vector.tensor_copy(v_w[a][b][:], tab_w[a][:].bitcast(U32).indirect(offs_t[:, 32 * b : 32 * b + 32]))
-
-        def gather_scales(b):
-            nc.vector.tensor_copy(v_s[b][:], tab_sc[:].indirect(offs_t[:, 32 * b : 32 * b + 32]))
-
-        def cast_w(a, r, on_scalar):
-            dst = w_bf[a, r][:].rearrange("p (t m j) -> p m t j", t=4, j=4)
-            src = w_raw[a, r][:].rearrange("p j (m t) -> p m t j", t=4)
-            if on_scalar:
+        def cast_w(a, r, eng, lo, hi):
+            dst = w_bf[a, r][:].rearrange("p (t m j) -> p m t j", t=4, j=4)[:, lo:hi]
+            src = w_raw[a, r, lo // 64][:].rearrange("p j (m t) -> p m t j", t=4)
+            if eng == "s":
                 nc.scalar.activation(dst, src, ACT.Copy, scale=-1.0)
+            elif eng == "g":
+                nc.gpsimd.tensor_scalar(dst, src, -1.0, 0.0, ALU.mult, ALU.add)
             else:
                 nc.vector.tensor_scalar(dst, src, -1.0, None, ALU.mult)
 
         def quant_w(a, r):
             nc.vector.quantize_mx(out=w_q[a, r][:].bitcast(FP8X4), scales=w_s[a, r][:], in_=w_bf[a, r][:])
 
-        gather_words(0, 0)
-        cast_w(0, 0, True)
-        gather_scales(0)
-        quant_w(0, 0)
-        gather_words(1, 0)
-        cast_w(1, 0, True)
-        quant_w(1, 0)
-        cast_w(0, 1, False)
-        quant_w(0, 1)
-        cast_w(1, 1, False)
-        quant_w(1, 1)
-        gather_words(0, 1)
-        gather_scales(1)
-        gather_words(1, 1)
-        nc.vector.tensor_scalar(
-            gpat[:], gain_t[:].unsqueeze(2).to_broadcast([P, 2, JC, 4]), -1.0, None, ALU.mult
-        )
+        nc.scalar.activation(warm[:], warm[:], ACT.Sigmoid)
+        for i, (a, r) in enumerate([(0, 0), (1, 0), (0, 1), (1, 1)]):
+            cast_w(a, r, CASTS[2 * i], 0, 64)
+            cast_w(a, r, CASTS[2 * i + 1], 64, 128)
+            quant_w(a, r)
+            if i == 0:
+                gather(0)
+        nc.vector.tensor_scalar(ngain[:], gain_t[:], -1.0, None, ALU.mult)
 
         banks = {}
+        free = list(range(8))
 
-        def first_product(r, c, slot):
+        def first_product(r, c):
+            slot = free.pop(0)
             bank = psum.tile([P, 4, JC], F32, name=f"a{r}{c}", tag=f"bank{slot}")
-            banks[r, c] = bank
-            b, cols = c // 4, slice(JC * (c % 4), JC * (c % 4 + 1))
+            banks[r, c] = (bank, slot)
+            b = [g for g in range(ng) if GATHERS[g][0] <= c < GATHERS[g][1]][0]
+            cols = slice(JC * (c - GATHERS[b][0]), JC * (c - GATHERS[b][0] + 1))
             for t in range(4):
                 for a in range(2):
                     nc.tensor.matmul_mx(
@@ -150,49 +155,71 @@ def tile_list_bond_softplus_store_kernel(
                         stop=(a == 1),
                     )
 
-        def sigmoid(r, c):
-            nc.scalar.activation(
-                sig[c][:, r, :].rearrange("p (j t) -> p j t", t=4),
-                banks[r, c][:].rearrange("p t j -> p j t"),
-                ACT.Sigmoid,
-            )
+        def batch(items, eps_on, chain):
+            for r, c in items:
+                first_product(r, c)
+                nc.scalar.activation(
+                    sig[c][:, r, :].rearrange("p (j t) -> p j t", t=4),
+                    banks[r, c][0][:].rearrange("p t j -> p j t"),
+                    ACT.Sigmoid,
+                )
+            lr, lc = items[-1]
+            eps_c = keep.tile([P, 1], F32, name=f"eps{lr}{lc}")
+            if eps_on == "g":
+                nc.gpsimd.tensor_scalar(eps_c[:], sig[lc][:, lr, 511:512], 0.0, EPS, ALU.mult, ALU.add)
+            else:
+                nc.scalar.activation(eps_c[:], sig[lc][:, lr, 511:512], ACT.Copy, scale=0.0, bias=EPS)
+            units = []
+            for r, c in items:
+                if (0, c) in items and (1, c) in items:
+                    if (c, 0, 2) not in units:
+                        units.append((c, 0, 2))
+                else:
+                    units.append((c, r, r + 1))
+            def log_guard(c, r0, r1):
+                flat = sig[c][:, r0:r1, :].rearrange("p r x -> p (r x)")
+                nc.scalar.activation(flat, flat, ACT.Ln, bias=eps_c[:], scale=2.0)
+                for r in range(r0, r1):
+                    view = sig[c][:, r, :].rearrange("p (j t) -> p j t", t=4)
+                    nc.vector.scalar_tensor_tensor(
+                        view, banks[r, c][0][:].rearrange("p t j -> p j t"), LN2, view, ALU.add, ALU.min
+                    )
+                    free.append(banks[r, c][1])
 
-        def log(c):
-            flat = sig[c][:].rearrange("p r x -> p (r x)")
-            nc.scalar.activation(flat, flat, ACT.Ln, bias=EPS, scale=2.0)
+            def gain_mul(c, r0, r1):
+                eng = nc.gpsimd if GAIN_ON[8 * r0 + c] == "g" else nc.vector
+                eng.tensor_tensor(
+                    h_bf[c][:, r0:r1, :].rearrange("p r (j t) -> p r j t", t=4),
+                    sig[c][:, r0:r1, :].rearrange("p r (j t) -> p r j t", t=4),
+                    ngain[:, r0:r1, :].unsqueeze(2).to_broadcast([P, r1 - r0, JC, 4]),
+                    ALU.mult,
+                )
 
-        def guard(r, c):
-            nc.vector.scalar_tensor_tensor(
-                u_t[c][:, r, :].rearrange("p (j t) -> p j t", t=4),
-                banks[r, c][:].rearrange("p t j -> p j t"),
-                LN2,
-                sig[c][:, r, :].rearrange("p (j t) -> p j t", t=4),
-                ALU.add,
-                ALU.min,
-            )
+            def quant_h(c, r0, r1):
+                nc.vector.quantize_mx(
+                    out=h_q[c][:, r0:r1, :].rearrange("p r j -> p (r j)").bitcast(FP8X4),
+                    scales=h_s[c][:, r0:r1, :].rearrange("p r j -> p (r j)"),
+                    in_=h_bf[c][:, r0:r1, :].rearrange("p r x -> p (r x)"),
+                )
 
-        def apply_gain(c):
-            eng = nc.gpsimd if GAIN_ON[c] == "g" else nc.vector
-            eng.tensor_tensor(
-                h_bf[c][:],
-                u_t[c][:].rearrange("p r x -> p (r x)"),
-                gpat[:].rearrange("p r j t -> p (r j t)"),
-                ALU.mult,
-            )
+            if chain:
+                for u in units:
+                    log_guard(*u)
+                    gain_mul(*u)
+                    quant_h(*u)
+            else:
+                for stage in (log_guard, gain_mul, quant_h):
+                    for u in units:
+                        stage(*u)
 
-        def quant_h(c):
-            nc.vector.quantize_mx(
-                out=h_q[c][:].rearrange("p r j -> p (r j)").bitcast(FP8X4),
-                scales=h_s[c][:].rearrange("p r j -> p (r j)"),
-                in_=h_bf[c][:],
-            )
-
-        def second_product(c, slot):
-            bank = psum.tile([P, 4, JC], F32, name=f"y{c}", tag=f"bank{slot}")
-            for q in range(4):
+        def second_product(g, q, pick):
+            lo, hi = GROUPS[g]
+            slot = free.pop(pick)
+            bank = psum.tile([P, 512], F32, name=f"y{g}{q}", tag=f"bank{slot}")
+            for c in range(lo, hi):
                 for r in range(2):
                     nc.tensor.matmul_mx(
-                        out=bank[:, q, :],
+                        out=bank[:, JC * (c - lo) : JC * (c - lo + 1)],
                         lhsT=w4_t[:, r, 256 * q : 256 * q + 256].bitcast(FP4X4),
                         lhsT_scale=w4_sc[:, r, 128 * q : 128 * q + 128],
                         rhs=h_q[c][:, r, :].bitcast(FP8X4),
@@ -200,62 +227,27 @@ def tile_list_bond_softplus_store_kernel(
                         start=(r == 0),
                         stop=(r == 1),
                     )
-            dst = yw[c // 2][:, :, JC * (c % 2) : JC * (c % 2 + 1)]
-            if SCATTER_TT:
-                nc.scalar.copy(dst, bank[:])
+            nc.scalar.copy(y_sb[g, q][:], bank[:, 0 : JC * (hi - lo)])
+            free.append(slot)
+            if not TT:
+                nc.gpsimd.tensor_tensor(y_sb[g, q][:], y_sb[g, q][:], wgo_t[:, JC * lo : JC * hi], ALU.mult)
+
+        def scatter(g, q):
+            lo, hi = GROUPS[g]
+            dst = win[q][:].indirect(offs2_t[:, 8 * lo : 8 * hi])
+            if TT:
+                nc.vector.tensor_tensor(dst, y_sb[g, q][:], wgo_t[:, JC * lo : JC * hi], ALU.mult)
             else:
-                nc.vector.tensor_tensor(
-                    dst, bank[:], wgo_t[:, JC * c : JC * (c + 1)].unsqueeze(1).to_broadcast([P, 4, JC]), ALU.mult
-                )
+                nc.vector.tensor_copy(dst, y_sb[g, q][:])
+            if g == len(GROUPS) - 1:
+                nc.sync.dma_start(out=out[128 * q : 128 * q + 128, :], in_=win[q][:])
 
-        def scatter(b, q):
-            dst = win[q][:].indirect(offs2_t[:, 16 * b : 16 * b + 16])
-            if SCATTER_TT:
-                nc.vector.tensor_tensor(dst, yw[b][:, q, :], wgo_t[:, 256 * b : 256 * b + 256], ALU.mult)
-            else:
-                nc.vector.tensor_copy(dst, yw[b][:, q, :])
-
-        nc.vector.memset(warm[:], 0.0)
-        nc.scalar.activation(warm[:], warm[:], ACT.Sigmoid)
-
-        for r in range(2):
-            for c in range(4):
-                first_product(r, c, 2 * c + r)
-                sigmoid(r, c)
-        for c in range(4):
-            log(c)
-            guard(0, c)
-            guard(1, c)
-        for c in range(4):
-            apply_gain(c)
-            quant_h(c)
-        for c in range(4, 7):
-            for r in range(2):
-                first_product(r, c, 2 * (c - 4) + r)
-        second_product(0, 6)
-        second_product(1, 7)
-        for r in range(2):
-            first_product(r, 7, 6 + r)
-        for c in range(4, 8):
-            for r in range(2):
-                sigmoid(r, c)
-        for q in range(4):
-            scatter(0, q)
-        for c in range(4, 8):
-            log(c)
-            guard(0, c)
-            guard(1, c)
-            if c == 4:
-                second_product(2, 0)
-                second_product(3, 1)
-        for q in range(4):
-            scatter(1, q)
-        for c in range(4, 8):
-            apply_gain(c)
-            quant_h(c)
-            second_product(c, 2 + c % 4)
-        for q in range(4):
-            scatter(2, q)
-        for q in range(4):
-            scatter(3, q)
-            nc.sync.dma_start(out=out[128 * q : 128 * q + 128, :], in_=win[q][:])
+        for step in PLAN:
+            if step[0] == "B":
+                batch(step[1], step[2][0], len(step[2]) > 1)
+            elif step[0] == "Y":
+                second_product(step[1], step[2], step[3])
+            elif step[0] == "S":
+                scatter(step[1], step[2])
+            elif step[0] == "G":
+                gather(step[1])

@@ -22,13 +22,13 @@ JC = 128
 NJC = S // JC
 EPS = 2.0**-60
 LN2 = math.log(2.0)
-PLAN = [('G', 1), ('B', [(0, 0), (0, 1), (0, 2), (0, 3), (0, 4), (0, 5), (1, 0), (1, 1)], 'g'), ('Y', 0, 0, 0), ('Y', 0, 1, 0), ('Y', 0, 2, 0), ('Y', 0, 3, 0), ('S', 0, 0), ('S', 0, 1), ('S', 0, 2), ('S', 0, 3), ('B', [(1, 2), (1, 3), (0, 6), (0, 7), (1, 4), (1, 5), (1, 6), (1, 7)], 'g'), ('Y', 1, 0, 0), ('Y', 1, 1, 0), ('Y', 1, 2, 0), ('Y', 1, 3, 0), ('Y', 2, 0, 0), ('Y', 2, 1, 0), ('Y', 2, 2, 0), ('Y', 2, 3, 0), ('S', 1, 0), ('S', 1, 1), ('S', 1, 2), ('S', 1, 3), ('S', 2, 0), ('S', 2, 1), ('S', 2, 2), ('S', 2, 3)]
-GROUPS = [(0, 2), (2, 4), (4, 8)]
-CASTS = 'sssvssvv'
-GAIN_ON = 'gvvvvvgvvvggvvvv'
+PLAN = [('B', [(0, 0), (0, 1), (0, 2), (0, 3), (0, 4), (0, 5)], 'g'), ('B', [(1, 0), (1, 1), (0, 6), (0, 7)], 'sc'), ('Y', 0, 0, 0), ('Y', 0, 1, 0), ('Y', 0, 2, 0), ('S', 0, 0), ('S', 0, 1), ('S', 0, 2), ('B', [(1, 2), (1, 3), (1, 4), (1, 5), (1, 6), (1, 7)], 's'), ('Y', 0, 3, -1), ('Y', 1, 0, 0), ('Y', 1, 1, 0), ('Y', 1, 2, 0), ('Y', 1, 3, 0), ('Y', 2, 0, 0), ('Y', 2, 1, 0), ('Y', 2, 2, 0), ('Y', 2, 3, 0), ('S', 0, 3), ('S', 1, 0), ('S', 1, 1), ('S', 1, 2), ('S', 1, 3), ('S', 2, 0), ('S', 2, 1), ('S', 2, 2), ('S', 2, 3)]
+GROUPS = [(0, 2), (2, 5), (5, 8)]
+CASTS = 'sssssvvv'
+GAIN_ON = 'ggvvvvvvvvgvvvvv'
 TT = True
-GATHERS = [(0, 3), (3, 8)]
-TABFIRST = True
+GATHERS = [(0, 8)]
+TABFIRST = False
 
 
 def tile_list_bond_softplus_store_kernel(
@@ -52,7 +52,7 @@ def tile_list_bond_softplus_store_kernel(
         w4_t = keep.tile([P, 2, 2 * N], U8, name="w4_t", align_bytes=64)
         wgo_t = keep.tile([P, S], F32, name="wgo_t")
         gain_t = keep.tile([P, 2, 4], F32, name="gain_t")
-        ngain = keep.tile([P, 2, 4], F32, name="ngain")
+        ngain = keep.tile([P, 2, JC, 4], F32, name="ngain")
         ng = len(GATHERS)
         v_w = [[keep.tile([P, JC * (hi - lo)], U32, name=f"v_w{a}{lo}", align_bytes=64) for lo, hi in GATHERS] for a in range(2)]
         v_s = [keep.tile([P, JC * (hi - lo)], U8, name=f"v_s{lo}", align_bytes=64) for lo, hi in GATHERS]
@@ -75,13 +75,14 @@ def tile_list_bond_softplus_store_kernel(
         def load_tab(a):
             nc.sync.dma_start(out=tab_w[a][:], in_=tab_words[a].rearrange("p t i -> p (t i)").bitcast(I32))
 
-        nc.gpsimd.memset(tab_sc[:].bitcast(I32), 0)
+        nc.vector.memset(tab_sc[:].bitcast(I32), 0)
         nc.vector.memset(warm[:], 0.0)
-        nc.gpsimd.memset(w4_sc[:].rearrange("p a n -> p (a n)").bitcast(I32), 0)
+        nc.vector.memset(w4_sc[:].rearrange("p a n -> p (a n)").bitcast(I32), 0)
         for q in range(4):
-            nc.gpsimd.memset(win[q][:].bitcast(I32), 0)
+            nc.vector.memset(win[q][:].bitcast(I32), 0)
         load_tab(0)
         nc.sync.dma_start(offs_t[:], offs)
+        nc.sync.dma_start(out=gain_t[:], in_=gain.rearrange("(a p t) -> p a t", a=2, t=4))
         for qd in range(4):
             nc.sync.dma_start(
                 out=tab_sc[32 * qd : 32 * qd + 8, :].bitcast(I32),
@@ -96,7 +97,6 @@ def tile_list_bond_softplus_store_kernel(
         load_w(1, 0)
         load_w(0, 1)
         load_w(1, 1)
-        nc.sync.dma_start(out=gain_t[:], in_=gain.rearrange("(a p t) -> p a t", a=2, t=4))
         for qd in range(4):
             nc.sync.dma_start(
                 out=w4_sc[32 * qd : 32 * qd + 4, :, :].bitcast(I32),
@@ -126,13 +126,15 @@ def tile_list_bond_softplus_store_kernel(
             nc.vector.quantize_mx(out=w_q[a, r][:].bitcast(FP8X4), scales=w_s[a, r][:], in_=w_bf[a, r][:])
 
         nc.scalar.activation(warm[:], warm[:], ACT.Sigmoid)
+        nc.scalar.activation(
+            ngain[:], gain_t[:].unsqueeze(2).to_broadcast([P, 2, JC, 4]), ACT.Copy, scale=-1.0
+        )
+        for g in range(ng):
+            gather(g)
         for i, (a, r) in enumerate([(0, 0), (1, 0), (0, 1), (1, 1)]):
             cast_w(a, r, CASTS[2 * i], 0, 64)
             cast_w(a, r, CASTS[2 * i + 1], 64, 128)
             quant_w(a, r)
-            if i == 0:
-                gather(0)
-        nc.vector.tensor_scalar(ngain[:], gain_t[:], -1.0, None, ALU.mult)
 
         banks = {}
         free = list(range(8))
@@ -189,9 +191,9 @@ def tile_list_bond_softplus_store_kernel(
             def gain_mul(c, r0, r1):
                 eng = nc.gpsimd if GAIN_ON[8 * r0 + c] == "g" else nc.vector
                 eng.tensor_tensor(
-                    h_bf[c][:, r0:r1, :].rearrange("p r (j t) -> p r j t", t=4),
-                    sig[c][:, r0:r1, :].rearrange("p r (j t) -> p r j t", t=4),
-                    ngain[:, r0:r1, :].unsqueeze(2).to_broadcast([P, r1 - r0, JC, 4]),
+                    h_bf[c][:, r0:r1, :].rearrange("p r x -> p (r x)"),
+                    sig[c][:, r0:r1, :].rearrange("p r x -> p (r x)"),
+                    ngain[:, r0:r1].rearrange("p r j t -> p (r j t)"),
                     ALU.mult,
                 )
 
@@ -249,5 +251,3 @@ def tile_list_bond_softplus_store_kernel(
                 second_product(step[1], step[2], step[3])
             elif step[0] == "S":
                 scatter(step[1], step[2])
-            elif step[0] == "G":
-                gather(step[1])

@@ -22,13 +22,13 @@ JC = 128
 NJC = S // JC
 EPS = 2.0**-60
 LN2 = math.log(2.0)
-PLAN = [('B', [(0, 0), (0, 1), (0, 2), (0, 3), (0, 4), (0, 5)], 'g'), ('B', [(1, 0), (1, 1), (0, 6), (0, 7)], 'sc'), ('Y', 0, 0, 0), ('Y', 0, 1, 0), ('Y', 0, 2, 0), ('S', 0, 0), ('S', 0, 1), ('S', 0, 2), ('B', [(1, 2), (1, 3), (1, 4), (1, 5), (1, 6), (1, 7)], 's'), ('Y', 0, 3, -1), ('Y', 1, 0, 0), ('Y', 1, 1, 0), ('Y', 1, 2, 0), ('Y', 1, 3, 0), ('Y', 2, 0, 0), ('Y', 2, 1, 0), ('Y', 2, 2, 0), ('Y', 2, 3, 0), ('S', 0, 3), ('S', 1, 0), ('S', 1, 1), ('S', 1, 2), ('S', 1, 3), ('S', 2, 0), ('S', 2, 1), ('S', 2, 2), ('S', 2, 3)]
+PLAN = [('B', [(0, 0), (0, 1), (0, 2), (0, 3), (0, 4), (0, 5)], 'g', 0, 2, 2, 2, 3), ('B', [(1, 0), (1, 1), (0, 6), (0, 7)], 's', 0, 1, 1, 1, 2), ('Y', 0, 0, 0), ('Y', 0, 1, 0), ('Y', 0, 2, 0), ('S', 0, 0), ('S', 0, 1), ('S', 0, 2), ('B', [(1, 2), (1, 3), (1, 4), (1, 5), (1, 6), (1, 7)], 's', 1, 1, 3, 4, 0), ('Y', 0, 3, -1), ('Y', 1, 0, 0), ('Y', 1, 1, 0), ('Y', 1, 2, 0), ('Y', 1, 3, 0), ('Y', 2, 0, 0), ('Y', 2, 1, 0), ('Y', 2, 2, 0), ('Y', 2, 3, 0), ('S', 0, 3), ('S', 1, 0), ('S', 1, 1), ('S', 1, 2), ('S', 1, 3), ('S', 2, 0), ('S', 2, 1), ('S', 2, 2), ('S', 2, 3)]
 GROUPS = [(0, 2), (2, 5), (5, 8)]
-CASTS = 'sssssvvv'
-GAIN_ON = 'ggvvvvvvvvgvvvvv'
+CASTS = 'ssssvvvv'
+GAIN_ON = 'vvvvvvvvvvvvvvvv'
 TT = True
-GATHERS = [(0, 8)]
-TABFIRST = False
+GATHERS = 6
+TABFIRST = 3
 
 
 def tile_list_bond_softplus_store_kernel(
@@ -45,7 +45,7 @@ def tile_list_bond_softplus_store_kernel(
         w4_sc = keep.tile([P, 2, N], U8, name="w4_sc", align_bytes=64)
         tab_w = [keep.tile([P, T], I32, name=f"tab_w{a}", align_bytes=64) for a in range(2)]
         ar = [(a, r) for a in range(2) for r in range(2)]
-        w_raw = {(a, r, u): keep.tile([P, 4, 256], F32, name=f"w_raw{a}{r}{u}") for a, r in ar for u in range(2)}
+        w_raw = {(a, r, u): keep.tile([P, 4, 512 // (a * r + 1)], F32, name=f"w_raw{a}{r}{u}") for a, r in ar for u in range(a * r + 1)}
         w_bf = {k: keep.tile([P, 2048], BF16, name=f"w_bf{k[0]}{k[1]}", align_bytes=64) for k in ar}
         w_q = {k: keep.tile([P, 512], U32, name=f"w_q{k[0]}{k[1]}", align_bytes=64) for k in ar}
         w_s = {k: keep.tile([P, 512], U8, name=f"w_s{k[0]}{k[1]}", align_bytes=64) for k in ar}
@@ -53,23 +53,32 @@ def tile_list_bond_softplus_store_kernel(
         wgo_t = keep.tile([P, S], F32, name="wgo_t")
         gain_t = keep.tile([P, 2, 4], F32, name="gain_t")
         ngain = keep.tile([P, 2, JC, 4], F32, name="ngain")
-        ng = len(GATHERS)
-        v_w = [[keep.tile([P, JC * (hi - lo)], U32, name=f"v_w{a}{lo}", align_bytes=64) for lo, hi in GATHERS] for a in range(2)]
-        v_s = [keep.tile([P, JC * (hi - lo)], U8, name=f"v_s{lo}", align_bytes=64) for lo, hi in GATHERS]
-        sig = [keep.tile([P, 2, 512], F32, name=f"sig{c}") for c in range(NJC)]
-        h_bf = [keep.tile([P, 2, 512], BF16, name=f"h_bf{c}", align_bytes=64) for c in range(NJC)]
-        h_q = [keep.tile([P, 2, JC], U32, name=f"h_q{c}", align_bytes=64) for c in range(NJC)]
-        h_s = [keep.tile([P, 2, JC], U8, name=f"h_s{c}", align_bytes=64) for c in range(NJC)]
+        cuts = {0: [(0, GATHERS), (GATHERS, 8)], 1: [(0, 2), (2, 4), (4, 6), (6, 8)], 2: [(0, 8)]}
+        v_t = {
+            (a, lo): keep.tile([P, JC * (hi - lo)], U32 if a < 2 else U8, name=f"v{a}{lo}", align_bytes=64)
+            for a in range(3)
+            for lo, hi in cuts[a]
+        }
+
+        def picked(a, c):
+            lo = [x for x, y in cuts[a] if x <= c < y][0]
+            return v_t[a, lo], slice(JC * (c - lo), JC * (c - lo + 1))
+
+        sig = [keep.tile([P, NJC * 512], F32, name=f"sig{r}") for r in range(2)]
+        h_bf = [keep.tile([P, NJC * 512], BF16, name=f"h_bf{r}", align_bytes=64) for r in range(2)]
+        h_q = [keep.tile([P, S], U32, name=f"h_q{r}", align_bytes=64) for r in range(2)]
+        h_s = [keep.tile([P, S], U8, name=f"h_s{r}", align_bytes=64) for r in range(2)]
         y_sb = {(g, q): keep.tile([P, JC * (GROUPS[g][1] - GROUPS[g][0])], F32, name=f"y{g}{q}") for g in range(len(GROUPS)) for q in range(4)}
         win = [keep.tile([P, T2], F32, name=f"win{q}") for q in range(4)]
         warm = keep.tile([P, 1], F32, name="warm")
 
         def load_w(a, r):
-            for u in range(2):
-                lo = 512 * r + 256 * u
+            wd = 512 // (a * r + 1)
+            for u in range(a * r + 1):
+                lo = 512 * r + wd * u
                 nc.sync.dma_start(
                     out=w_raw[a, r, u][:],
-                    in_=w1[512 * a : 512 * a + 512, lo : lo + 256].rearrange("(p j) c -> p j c", j=4),
+                    in_=w1[512 * a : 512 * a + 512, lo : lo + wd].rearrange("(p j) c -> p j c", j=4),
                 )
 
         def load_tab(a):
@@ -80,21 +89,17 @@ def tile_list_bond_softplus_store_kernel(
         nc.vector.memset(w4_sc[:].rearrange("p a n -> p (a n)").bitcast(I32), 0)
         for q in range(4):
             nc.vector.memset(win[q][:].bitcast(I32), 0)
-        load_tab(0)
-        nc.sync.dma_start(offs_t[:], offs)
         nc.sync.dma_start(out=gain_t[:], in_=gain.rearrange("(a p t) -> p a t", a=2, t=4))
+        nc.sync.dma_start(offs_t[:], offs)
+        load_w(0, 0)
         for qd in range(4):
             nc.sync.dma_start(
                 out=tab_sc[32 * qd : 32 * qd + 8, :].bitcast(I32),
                 in_=tab_scales[:, 4 * qd : 4 * qd + 4, :].bitcast(I32),
             )
-        if TABFIRST:
-            load_tab(1)
-            load_w(0, 0)
-        else:
-            load_w(0, 0)
-            load_tab(1)
         load_w(1, 0)
+        load_tab(0)
+        load_tab(1)
         load_w(0, 1)
         load_w(1, 1)
         for qd in range(4):
@@ -106,15 +111,17 @@ def tile_list_bond_softplus_store_kernel(
         nc.sync.dma_start(out=wgo_t[:], in_=wgo)
         nc.sync.dma_start(offs2_t[:], offs2)
 
-        def gather(g):
-            cols = slice(8 * GATHERS[g][0], 8 * GATHERS[g][1])
-            nc.vector.tensor_copy(v_w[0][g][:], tab_w[0][:].bitcast(U32).indirect(offs_t[:, cols]))
-            nc.vector.tensor_copy(v_s[g][:], tab_sc[:].indirect(offs_t[:, cols]))
-            nc.vector.tensor_copy(v_w[1][g][:], tab_w[1][:].bitcast(U32).indirect(offs_t[:, cols]))
+        def gather(a, i):
+            lo, hi = cuts[a][i]
+            src = tab_w[a][:].bitcast(U32) if a < 2 else tab_sc[:]
+            nc.vector.tensor_copy(v_t[a, lo][:], src.indirect(offs_t[:, 8 * lo : 8 * hi]))
 
         def cast_w(a, r, eng, lo, hi):
             dst = w_bf[a, r][:].rearrange("p (t m j) -> p m t j", t=4, j=4)[:, lo:hi]
-            src = w_raw[a, r, lo // 64][:].rearrange("p j (m t) -> p m t j", t=4)
+            if a * r == 0:
+                src = w_raw[a, r, 0][:].rearrange("p j (m t) -> p m t j", t=4)[:, lo:hi]
+            else:
+                src = w_raw[a, r, lo // 64][:].rearrange("p j (m t) -> p m t j", t=4)
             if eng == "s":
                 nc.scalar.activation(dst, src, ACT.Copy, scale=-1.0)
             elif eng == "g":
@@ -129,12 +136,26 @@ def tile_list_bond_softplus_store_kernel(
         nc.scalar.activation(
             ngain[:], gain_t[:].unsqueeze(2).to_broadcast([P, 2, JC, 4]), ACT.Copy, scale=-1.0
         )
-        for g in range(ng):
-            gather(g)
-        for i, (a, r) in enumerate([(0, 0), (1, 0), (0, 1), (1, 1)]):
-            cast_w(a, r, CASTS[2 * i], 0, 64)
-            cast_w(a, r, CASTS[2 * i + 1], 64, 128)
+        def prep(i):
+            a, r = i % 2, i // 2
+            if a * r == 0 and CASTS[2 * i] == CASTS[2 * i + 1]:
+                cast_w(a, r, CASTS[2 * i], 0, 128)
+            else:
+                cast_w(a, r, CASTS[2 * i], 0, 64)
+                cast_w(a, r, CASTS[2 * i + 1], 64, 128)
             quant_w(a, r)
+
+        gather(2, 0)
+        prep(0)
+        gather(0, 0)
+        prep(1)
+        for i in range(TABFIRST):
+            gather(1, i)
+        gather(0, 1)
+        for i in range(TABFIRST, 4):
+            gather(1, i)
+        prep(2)
+        prep(3)
 
         banks = {}
         free = list(range(8))
@@ -143,76 +164,83 @@ def tile_list_bond_softplus_store_kernel(
             slot = free.pop(0)
             bank = psum.tile([P, 4, JC], F32, name=f"a{r}{c}", tag=f"bank{slot}")
             banks[r, c] = (bank, slot)
-            b = [g for g in range(ng) if GATHERS[g][0] <= c < GATHERS[g][1]][0]
-            cols = slice(JC * (c - GATHERS[b][0]), JC * (c - GATHERS[b][0] + 1))
             for t in range(4):
                 for a in range(2):
                     nc.tensor.matmul_mx(
                         out=bank[:, t, :],
                         lhsT=w_q[a, r][:, 128 * t : 128 * t + 128].bitcast(FP8X4),
                         lhsT_scale=w_s[a, r][:, 128 * t : 128 * t + 128],
-                        rhs=v_w[a][b][:, cols].bitcast(FP8X4),
-                        rhs_scale=v_s[b][4 * a : 128, cols],
+                        rhs=picked(a, c)[0][:, picked(a, c)[1]].bitcast(FP8X4),
+                        rhs_scale=picked(2, c)[0][4 * a : 128, picked(2, c)[1]],
                         start=(a == 0),
                         stop=(a == 1),
                     )
 
-        def batch(items, eps_on, chain):
+        def runs(items, width):
+            res = []
+            for r, c in items:
+                if res and res[-1][0] == r and res[-1][2] == c and res[-1][2] - res[-1][1] < width:
+                    res[-1] = (r, res[-1][1], c + 1)
+                else:
+                    res.append((r, c, c + 1))
+            return res
+
+        def batch(items, eps_on, ngp, lw, gw, qw, early):
             for r, c in items:
                 first_product(r, c)
                 nc.scalar.activation(
-                    sig[c][:, r, :].rearrange("p (j t) -> p j t", t=4),
+                    sig[r][:, 512 * c : 512 * c + 512].rearrange("p (j t) -> p j t", t=4),
                     banks[r, c][0][:].rearrange("p t j -> p j t"),
                     ACT.Sigmoid,
                 )
             lr, lc = items[-1]
             eps_c = keep.tile([P, 1], F32, name=f"eps{lr}{lc}")
+            last = sig[lr][:, 512 * lc + 511 : 512 * lc + 512]
             if eps_on == "g":
-                nc.gpsimd.tensor_scalar(eps_c[:], sig[lc][:, lr, 511:512], 0.0, EPS, ALU.mult, ALU.add)
+                nc.gpsimd.tensor_scalar(eps_c[:], last, 0.0, EPS, ALU.mult, ALU.add)
             else:
-                nc.scalar.activation(eps_c[:], sig[lc][:, lr, 511:512], ACT.Copy, scale=0.0, bias=EPS)
-            units = []
-            for r, c in items:
-                if (0, c) in items and (1, c) in items:
-                    if (c, 0, 2) not in units:
-                        units.append((c, 0, 2))
-                else:
-                    units.append((c, r, r + 1))
-            def log_guard(c, r0, r1):
-                flat = sig[c][:, r0:r1, :].rearrange("p r x -> p (r x)")
-                nc.scalar.activation(flat, flat, ACT.Ln, bias=eps_c[:], scale=2.0)
-                for r in range(r0, r1):
-                    view = sig[c][:, r, :].rearrange("p (j t) -> p j t", t=4)
-                    nc.vector.scalar_tensor_tensor(
-                        view, banks[r, c][0][:].rearrange("p t j -> p j t"), LN2, view, ALU.add, ALU.min
-                    )
-                    free.append(banks[r, c][1])
+                nc.scalar.activation(eps_c[:], last, ACT.Copy, scale=0.0, bias=EPS)
 
-            def gain_mul(c, r0, r1):
-                eng = nc.gpsimd if GAIN_ON[8 * r0 + c] == "g" else nc.vector
-                eng.tensor_tensor(
-                    h_bf[c][:, r0:r1, :].rearrange("p r x -> p (r x)"),
-                    sig[c][:, r0:r1, :].rearrange("p r x -> p (r x)"),
-                    ngain[:, r0:r1].rearrange("p r j t -> p (r j t)"),
-                    ALU.mult,
-                )
+            def log_guard(part):
+                for r, c0, c1 in runs(part, lw):
+                    flat = sig[r][:, 512 * c0 : 512 * c1]
+                    nc.scalar.activation(flat, flat, ACT.Ln, bias=eps_c[:], scale=2.0)
+                    for c in range(c0, c1):
+                        view = sig[r][:, 512 * c : 512 * c + 512].rearrange("p (j t) -> p j t", t=4)
+                        nc.vector.scalar_tensor_tensor(
+                            view, banks[r, c][0][:].rearrange("p t j -> p j t"), LN2, view, ALU.add, ALU.min
+                        )
+                        free.append(banks[r, c][1])
 
-            def quant_h(c, r0, r1):
-                nc.vector.quantize_mx(
-                    out=h_q[c][:, r0:r1, :].rearrange("p r j -> p (r j)").bitcast(FP8X4),
-                    scales=h_s[c][:, r0:r1, :].rearrange("p r j -> p (r j)"),
-                    in_=h_bf[c][:, r0:r1, :].rearrange("p r x -> p (r x)"),
-                )
+            def gain_quant(part):
+                on_g = [x for x in part if x in items[:ngp]]
+                on_v = [x for x in part if x not in items[:ngp]]
+                for eng, sub, wd in ((nc.gpsimd, on_g, 1), (nc.vector, on_v, gw)):
+                    for r, c0, c1 in runs(sub, wd):
+                        eng.tensor_tensor(
+                            h_bf[r][:, 512 * c0 : 512 * c1].rearrange("p (c x) -> p c x", x=512),
+                            sig[r][:, 512 * c0 : 512 * c1].rearrange("p (c x) -> p c x", x=512),
+                            ngain[:, r : r + 1].rearrange("p r j t -> p r (j t)").to_broadcast([P, c1 - c0, 512]),
+                            ALU.mult,
+                        )
+                for r, c0, c1 in runs(part, qw):
+                    if c1 - c0 == 3:
+                        pieces = [(c0, c0 + 2), (c0 + 2, c1)]
+                    else:
+                        pieces = [(c0, c1)]
+                    for d0, d1 in pieces:
+                        nc.vector.quantize_mx(
+                            out=h_q[r][:, JC * d0 : JC * d1].bitcast(FP8X4),
+                            scales=h_s[r][:, JC * d0 : JC * d1],
+                            in_=h_bf[r][:, 512 * d0 : 512 * d1],
+                        )
 
-            if chain:
-                for u in units:
-                    log_guard(*u)
-                    gain_mul(*u)
-                    quant_h(*u)
-            else:
-                for stage in (log_guard, gain_mul, quant_h):
-                    for u in units:
-                        stage(*u)
+            for part in (items[:early], items[early:]):
+                log_guard(part)
+                if early:
+                    gain_quant(part)
+            if not early:
+                gain_quant(items)
 
         def second_product(g, q, pick):
             lo, hi = GROUPS[g]
@@ -224,8 +252,8 @@ def tile_list_bond_softplus_store_kernel(
                         out=bank[:, JC * (c - lo) : JC * (c - lo + 1)],
                         lhsT=w4_t[:, r, 256 * q : 256 * q + 256].bitcast(FP4X4),
                         lhsT_scale=w4_sc[:, r, 128 * q : 128 * q + 128],
-                        rhs=h_q[c][:, r, :].bitcast(FP8X4),
-                        rhs_scale=h_s[c][:, r, :],
+                        rhs=h_q[r][:, JC * c : JC * c + JC].bitcast(FP8X4),
+                        rhs_scale=h_s[r][:, JC * c : JC * c + JC],
                         start=(r == 0),
                         stop=(r == 1),
                     )
@@ -246,7 +274,7 @@ def tile_list_bond_softplus_store_kernel(
 
         for step in PLAN:
             if step[0] == "B":
-                batch(step[1], step[2][0], len(step[2]) > 1)
+                batch(*step[1:])
             elif step[0] == "Y":
                 second_product(step[1], step[2], step[3])
             elif step[0] == "S":

@@ -2,6 +2,7 @@ import math
 from contextlib import ExitStack
 
 import concourse.mybir as mybir
+from concourse.masks import make_identity
 
 K, H, N, T, S, T2 = 1024, 1024, 512, 2048, 1024, 2048
 FLOPS = 2 * K * H * S + 2 * H * N * S
@@ -22,13 +23,6 @@ JC = 128
 NJC = S // JC
 EPS = 2.0**-60
 LN2 = math.log(2.0)
-PLAN = [('B', [(0, 0), (0, 1), (0, 2), (0, 3), (0, 4), (0, 5)], 'g', 0, 2, 2, 2, 3), ('B', [(1, 0), (1, 1), (0, 6), (0, 7)], 's', 0, 1, 1, 1, 2), ('Y', 0, 0, 0), ('Y', 0, 1, 0), ('Y', 0, 2, 0), ('S', 0, 0), ('S', 0, 1), ('S', 0, 2), ('B', [(1, 2), (1, 3), (1, 4), (1, 5), (1, 6), (1, 7)], 's', 1, 1, 3, 4, 0), ('Y', 0, 3, -1), ('Y', 1, 0, 0), ('Y', 1, 1, 0), ('Y', 1, 2, 0), ('Y', 1, 3, 0), ('Y', 2, 0, 0), ('Y', 2, 1, 0), ('Y', 2, 2, 0), ('Y', 2, 3, 0), ('S', 0, 3), ('S', 1, 0), ('S', 1, 1), ('S', 1, 2), ('S', 1, 3), ('S', 2, 0), ('S', 2, 1), ('S', 2, 2), ('S', 2, 3)]
-GROUPS = [(0, 2), (2, 5), (5, 8)]
-CASTS = 'ssssvvvv'
-GAIN_ON = 'vvvvvvvvvvvvvvvv'
-TT = True
-GATHERS = 6
-TABFIRST = 3
 
 
 def tile_list_bond_softplus_store_kernel(
@@ -37,6 +31,7 @@ def tile_list_bond_softplus_store_kernel(
     nc = tc.nc
     with ExitStack() as ctx:
         keep = ctx.enter_context(tc.tile_pool(name="keep", bufs=1))
+        reuse = ctx.enter_context(tc.tile_pool(name="reuse", bufs=1))
         psum = ctx.enter_context(tc.psum_pool(name="psum", bufs=1))
 
         offs_t = keep.tile([P, S // 16], U16, name="offs_t")
@@ -44,37 +39,42 @@ def tile_list_bond_softplus_store_kernel(
         tab_sc = keep.tile([P, T], U8, name="tab_sc", align_bytes=64)
         w4_sc = keep.tile([P, 2, N], U8, name="w4_sc", align_bytes=64)
         tab_w = [keep.tile([P, T], I32, name=f"tab_w{a}", align_bytes=64) for a in range(2)]
-        ar = [(a, r) for a in range(2) for r in range(2)]
-        w_raw = {(a, r, u): keep.tile([P, 4, 512 // (a * r + 1)], F32, name=f"w_raw{a}{r}{u}") for a, r in ar for u in range(a * r + 1)}
-        w_bf = {k: keep.tile([P, 2048], BF16, name=f"w_bf{k[0]}{k[1]}", align_bytes=64) for k in ar}
+        ar = [(a, r) for r in range(2) for a in range(2)]
+        w_raw = {(0, r, 0): keep.tile([P, 4, 512], F32, name=f"w_raw0{r}") for r in range(2)}
+        for u in range(2):
+            w_raw[1, 0, u] = keep.tile([P, 4, 256], F32, name=f"w_raw10{u}")
+        w_raw[1, 1, 0] = keep.tile([P, 4, 256], F32, name="w_raw110")
+        w_raw[1, 1, 1] = keep.tile([P, 4, 256], F32, name="w_raw111")
+        w_bf = {k: keep.tile([P, 2048], BF16, name=f"w_bf{k[0]}{k[1]}", tag=f"bf{i}", align_bytes=64) for i, k in enumerate(ar[:3])}
+        w_bf[1, 1] = reuse.tile([P, 2048], BF16, name="w_bf11", offset=6144, align_bytes=64)
         w_q = {k: keep.tile([P, 512], U32, name=f"w_q{k[0]}{k[1]}", align_bytes=64) for k in ar}
         w_s = {k: keep.tile([P, 512], U8, name=f"w_s{k[0]}{k[1]}", align_bytes=64) for k in ar}
         w4_t = keep.tile([P, 2, 2 * N], U8, name="w4_t", align_bytes=64)
         wgo_t = keep.tile([P, S], F32, name="wgo_t")
         gain_t = keep.tile([P, 2, 4], F32, name="gain_t")
         ngain = keep.tile([P, 2, JC, 4], F32, name="ngain")
-        cuts = {0: [(0, GATHERS), (GATHERS, 8)], 1: [(0, 2), (2, 4), (4, 6), (6, 8)], 2: [(0, 8)]}
-        v_t = {
-            (a, lo): keep.tile([P, JC * (hi - lo)], U32 if a < 2 else U8, name=f"v{a}{lo}", align_bytes=64)
-            for a in range(3)
-            for lo, hi in cuts[a]
+        cuts = [[(0, 8)], [(0, 2), (2, 6), (6, 8)]]
+        v_w = {(a, lo): keep.tile([P, JC * (hi - lo)], U32, name=f"v{a}{lo}", align_bytes=64) for a in range(2) for lo, hi in cuts[a][:2]}
+        v_w[1, 6] = reuse.tile([P, 2 * JC], U32, name="v16", offset=8192, align_bytes=64)
+        v_s = [
+            keep.tile([P, 6 * JC], U8, name="v_s0", align_bytes=64),
+            reuse.tile([P, 2 * JC], U8, name="v_s1", offset=9216, align_bytes=64),
+        ]
+        rc = [(r, c) for r in range(2) for c in range(NJC)]
+        sig = {k: keep.tile([P, 512], F32, name=f"sig{k[0]}{k[1]}") for k in rc}
+        late = reuse.tile([P, 4, 512], F32, name="nega_late", offset=0, align_bytes=64)
+        nega = {
+            (r, c): late[:, c - 2] if r == 0 and 2 <= c < 6 else keep.tile([P, 512], F32, name=f"nega{r}{c}")[:]
+            for r, c in rc
         }
-
-        def picked(a, c):
-            lo = [x for x, y in cuts[a] if x <= c < y][0]
-            return v_t[a, lo], slice(JC * (c - lo), JC * (c - lo + 1))
-
-        sig = [keep.tile([P, NJC * 512], F32, name=f"sig{r}") for r in range(2)]
-        h_bf = [keep.tile([P, NJC * 512], BF16, name=f"h_bf{r}", align_bytes=64) for r in range(2)]
-        h_q = [keep.tile([P, S], U32, name=f"h_q{r}", align_bytes=64) for r in range(2)]
-        h_s = [keep.tile([P, S], U8, name=f"h_s{r}", align_bytes=64) for r in range(2)]
-        y_sb = {(g, q): keep.tile([P, JC * (GROUPS[g][1] - GROUPS[g][0])], F32, name=f"y{g}{q}") for g in range(len(GROUPS)) for q in range(4)}
+        ident = keep.tile([P, P], F32, name="ident")
+        h_q = {(r, half): keep.tile([P, 4 * JC], U32, name=f"h_q{r}{half}", align_bytes=64) for r in range(2) for half in range(2)}
+        h_s = {(r, half): keep.tile([P, 4 * JC], U8, name=f"h_s{r}{half}", align_bytes=64) for r in range(2) for half in range(2)}
         win = [keep.tile([P, T2], F32, name=f"win{q}") for q in range(4)]
-        warm = keep.tile([P, 1], F32, name="warm")
 
         def load_w(a, r):
-            wd = 512 // (a * r + 1)
-            for u in range(a * r + 1):
+            wd = 512 // (a + 1)
+            for u in range(a + 1):
                 lo = 512 * r + wd * u
                 nc.sync.dma_start(
                     out=w_raw[a, r, u][:],
@@ -85,23 +85,21 @@ def tile_list_bond_softplus_store_kernel(
             nc.sync.dma_start(out=tab_w[a][:], in_=tab_words[a].rearrange("p t i -> p (t i)").bitcast(I32))
 
         nc.vector.memset(tab_sc[:].bitcast(I32), 0)
-        nc.vector.memset(warm[:], 0.0)
-        nc.vector.memset(w4_sc[:].rearrange("p a n -> p (a n)").bitcast(I32), 0)
-        for q in range(4):
-            nc.vector.memset(win[q][:].bitcast(I32), 0)
-        nc.sync.dma_start(out=gain_t[:], in_=gain.rearrange("(a p t) -> p a t", a=2, t=4))
         nc.sync.dma_start(offs_t[:], offs)
-        load_w(0, 0)
+        nc.sync.dma_start(offs2_t[:], offs2)
+        nc.sync.dma_start(out=gain_t[:], in_=gain.rearrange("(a p t) -> p a t", a=2, t=4))
+        load_tab(0)
         for qd in range(4):
             nc.sync.dma_start(
                 out=tab_sc[32 * qd : 32 * qd + 8, :].bitcast(I32),
                 in_=tab_scales[:, 4 * qd : 4 * qd + 4, :].bitcast(I32),
             )
+        load_w(0, 0)
         load_w(1, 0)
-        load_tab(0)
         load_tab(1)
         load_w(0, 1)
         load_w(1, 1)
+        nc.vector.memset(w4_sc[:].rearrange("p a n -> p (a n)").bitcast(I32), 0)
         for qd in range(4):
             nc.sync.dma_start(
                 out=w4_sc[32 * qd : 32 * qd + 4, :, :].bitcast(I32),
@@ -109,173 +107,151 @@ def tile_list_bond_softplus_store_kernel(
             )
         nc.sync.dma_start(out=w4_t[:].bitcast(I32), in_=w4_words.rearrange("a p n -> p a n").bitcast(I32))
         nc.sync.dma_start(out=wgo_t[:], in_=wgo)
-        nc.sync.dma_start(offs2_t[:], offs2)
 
-        def gather(a, i):
-            lo, hi = cuts[a][i]
-            src = tab_w[a][:].bitcast(U32) if a < 2 else tab_sc[:]
-            nc.vector.tensor_copy(v_t[a, lo][:], src.indirect(offs_t[:, 8 * lo : 8 * hi]))
+        def gather(a, lo, hi):
+            nc.vector.tensor_copy(v_w[a, lo][:], tab_w[a][:].bitcast(U32).indirect(offs_t[:, 8 * lo : 8 * hi]))
 
-        def cast_w(a, r, eng, lo, hi):
-            dst = w_bf[a, r][:].rearrange("p (t m j) -> p m t j", t=4, j=4)[:, lo:hi]
-            if a * r == 0:
-                src = w_raw[a, r, 0][:].rearrange("p j (m t) -> p m t j", t=4)[:, lo:hi]
-            else:
-                src = w_raw[a, r, lo // 64][:].rearrange("p j (m t) -> p m t j", t=4)
-            if eng == "s":
-                nc.scalar.activation(dst, src, ACT.Copy, scale=-1.0)
-            elif eng == "g":
-                nc.gpsimd.tensor_scalar(dst, src, -1.0, 0.0, ALU.mult, ALU.add)
-            else:
-                nc.vector.tensor_scalar(dst, src, -1.0, None, ALU.mult)
-
-        def quant_w(a, r):
+        def prep(a, r):
+            wd = 2048 // (a + 1)
+            for u in range(a + 1):
+                src = w_raw[a, r, u][:].rearrange("p j (m i) -> p m j i", i=4)
+                dst = w_bf[a, r][:, wd * u : wd * (u + 1)].rearrange("p (m i j) -> p m j i", i=4, j=4)
+                if r == 0 and u == 0:
+                    nc.scalar.copy(dst, src)
+                else:
+                    nc.vector.tensor_copy(dst, src)
             nc.vector.quantize_mx(out=w_q[a, r][:].bitcast(FP8X4), scales=w_s[a, r][:], in_=w_bf[a, r][:])
 
-        nc.scalar.activation(warm[:], warm[:], ACT.Sigmoid)
-        nc.scalar.activation(
-            ngain[:], gain_t[:].unsqueeze(2).to_broadcast([P, 2, JC, 4]), ACT.Copy, scale=-1.0
-        )
-        def prep(i):
-            a, r = i % 2, i // 2
-            if a * r == 0 and CASTS[2 * i] == CASTS[2 * i + 1]:
-                cast_w(a, r, CASTS[2 * i], 0, 128)
-            else:
-                cast_w(a, r, CASTS[2 * i], 0, 64)
-                cast_w(a, r, CASTS[2 * i + 1], 64, 128)
-            quant_w(a, r)
-
-        gather(2, 0)
-        prep(0)
-        gather(0, 0)
-        prep(1)
-        for i in range(TABFIRST):
-            gather(1, i)
-        gather(0, 1)
-        for i in range(TABFIRST, 4):
-            gather(1, i)
-        prep(2)
-        prep(3)
+        make_identity(nc, ident[:])
+        gather(0, 0, 8)
+        nc.vector.tensor_copy(v_s[0][:], tab_sc[:].indirect(offs_t[:, 0:48]))
+        prep(0, 0)
+        prep(1, 0)
+        gather(1, 0, 2)
+        gather(1, 2, 6)
+        prep(0, 1)
+        prep(1, 1)
+        nc.scalar.activation(ngain[:], gain_t[:].unsqueeze(2).to_broadcast([P, 2, JC, 4]), ACT.Copy, scale=-1.0)
 
         banks = {}
-        free = list(range(8))
 
-        def first_product(r, c):
-            slot = free.pop(0)
-            bank = psum.tile([P, 4, JC], F32, name=f"a{r}{c}", tag=f"bank{slot}")
-            banks[r, c] = (bank, slot)
+        def first_pass(r, c, a):
+            lo = max(x for x, y in cuts[a] if x <= c)
+            nc.tensor.matmul_mx(
+                out=banks[r, c][:],
+                lhsT=v_w[a, lo][:, JC * (c - lo) : JC * (c - lo + 1)].bitcast(FP8X4),
+                lhsT_scale=v_s[c // 6][4 * a : 128, JC * (c % 6) : JC * (c % 6 + 1)],
+                rhs=w_q[a, r][:].bitcast(FP8X4),
+                rhs_scale=w_s[a, r][:],
+                start=(a == 0),
+                stop=(a == 1),
+            )
+
+        def read_a(r, c, copy_on_scalar):
+            by_t = banks[r, c][:].rearrange("p (m t) -> p t m", t=4)
+            nc.scalar.activation(sig[r, c][:].rearrange("p (t m) -> p t m", t=4), by_t, ACT.Sigmoid)
+            dst = nega[r, c].rearrange("p (t m) -> p t m", t=4)
+            if copy_on_scalar:
+                nc.scalar.activation(dst, by_t, ACT.Copy, scale=-1.0)
+            else:
+                nc.vector.tensor_scalar(dst, by_t, -1.0, None, ALU.mult)
+
+        def eps_after(r, c):
+            eps_c = keep.tile([P, 1], F32, name=f"eps{r}{c}")
+            nc.scalar.activation(eps_c[:], sig[r, c][:, 511:512], ACT.Copy, scale=0.0, bias=EPS)
+            return eps_c
+
+        def turn(u, src, first):
             for t in range(4):
-                for a in range(2):
-                    nc.tensor.matmul_mx(
-                        out=bank[:, t, :],
-                        lhsT=w_q[a, r][:, 128 * t : 128 * t + 128].bitcast(FP8X4),
-                        lhsT_scale=w_s[a, r][:, 128 * t : 128 * t + 128],
-                        rhs=picked(a, c)[0][:, picked(a, c)[1]].bitcast(FP8X4),
-                        rhs_scale=picked(2, c)[0][4 * a : 128, picked(2, c)[1]],
-                        start=(a == 0),
-                        stop=(a == 1),
-                    )
-
-        def runs(items, width):
-            res = []
-            for r, c in items:
-                if res and res[-1][0] == r and res[-1][2] == c and res[-1][2] - res[-1][1] < width:
-                    res[-1] = (r, res[-1][1], c + 1)
-                else:
-                    res.append((r, c, c + 1))
-            return res
-
-        def batch(items, eps_on, ngp, lw, gw, qw, early):
-            for r, c in items:
-                first_product(r, c)
-                nc.scalar.activation(
-                    sig[r][:, 512 * c : 512 * c + 512].rearrange("p (j t) -> p j t", t=4),
-                    banks[r, c][0][:].rearrange("p t j -> p j t"),
-                    ACT.Sigmoid,
+                nc.tensor.matmul(
+                    u[:, t, :], src[:, 128 * t : 128 * t + 128], ident[:],
+                    start=(first and t == 0), stop=(not first and t == 3), is_transpose=True,
                 )
-            lr, lc = items[-1]
-            eps_c = keep.tile([P, 1], F32, name=f"eps{lr}{lc}")
-            last = sig[lr][:, 512 * lc + 511 : 512 * lc + 512]
-            if eps_on == "g":
-                nc.gpsimd.tensor_scalar(eps_c[:], last, 0.0, EPS, ALU.mult, ALU.add)
-            else:
-                nc.scalar.activation(eps_c[:], last, ACT.Copy, scale=0.0, bias=EPS)
 
-            def log_guard(part):
-                for r, c0, c1 in runs(part, lw):
-                    flat = sig[r][:, 512 * c0 : 512 * c1]
-                    nc.scalar.activation(flat, flat, ACT.Ln, bias=eps_c[:], scale=2.0)
-                    for c in range(c0, c1):
-                        view = sig[r][:, 512 * c : 512 * c + 512].rearrange("p (j t) -> p j t", t=4)
-                        nc.vector.scalar_tensor_tensor(
-                            view, banks[r, c][0][:].rearrange("p t j -> p j t"), LN2, view, ALU.add, ALU.min
+        def finish_h(r, g, eps_c, slots):
+            h_bf = keep.tile([P, 2048], BF16, name=f"h_bf{r}{g}", tag=f"bf{g}", align_bytes=64)
+            for i in range(2):
+                c = 2 * g + i
+                u = psum.tile([P, 4, JC], F32, name=f"u{r}{c}", tag=f"bank{slots[i]}")
+                turn(u, nega[r, c], True)
+                nc.scalar.activation(sig[r, c][:], sig[r, c][:], ACT.Ln, bias=eps_c[:], scale=2.0)
+                turn(u, sig[r, c], False)
+                nc.vector.scalar_tensor_tensor(
+                    h_bf[:, 512 * i : 512 * i + 512].rearrange("p (j t) -> p j t", t=4),
+                    u[:].rearrange("p t j -> p j t"),
+                    LN2,
+                    ngain[:, r],
+                    ALU.min,
+                    ALU.mult,
+                )
+            cols = slice(2 * JC * (g % 2), 2 * JC * (g % 2 + 1))
+            nc.vector.quantize_mx(
+                out=h_q[r, g // 2][:, cols].bitcast(FP8X4), scales=h_s[r, g // 2][:, cols], in_=h_bf[:, 0:1024]
+            )
+
+        def second_product(parts, slot):
+            name = "y" + "".join(f"{q}{lo}" for q, lo, hi in parts)
+            bank = psum.tile([P, 512], F32, name=name, tag=f"bank{slot}")
+            wd = 512 if len(parts) == 1 else JC
+            at = 0
+            for q, lo, hi in parts:
+                for c0 in range(lo, hi, wd):
+                    cols = slice(c0 % 512, c0 % 512 + wd)
+                    for r in range(2):
+                        nc.tensor.matmul_mx(
+                            out=bank[:, at : at + wd],
+                            lhsT=w4_t[:, r, 256 * q : 256 * q + 256].bitcast(FP4X4),
+                            lhsT_scale=w4_sc[:, r, 128 * q : 128 * q + 128],
+                            rhs=h_q[r, lo // 512][:, cols].bitcast(FP8X4),
+                            rhs_scale=h_s[r, lo // 512][:, cols],
+                            start=(r == 0),
+                            stop=(r == 1),
                         )
-                        free.append(banks[r, c][1])
+                    at += wd
+            y = keep.tile([P, 512], F32, name="s" + name)
+            nc.scalar.copy(y[:], bank[:])
+            at = 0
+            for q, lo, hi in parts:
+                nc.vector.tensor_tensor(
+                    win[q][:].indirect(offs2_t[:, lo // 16 : hi // 16]), y[:, at : at + hi - lo], wgo_t[:, lo:hi], ALU.mult
+                )
+                at += hi - lo
+                if hi == S:
+                    nc.sync.dma_start(out=out[128 * q : 128 * q + 128, :], in_=win[q][:])
 
-            def gain_quant(part):
-                on_g = [x for x in part if x in items[:ngp]]
-                on_v = [x for x in part if x not in items[:ngp]]
-                for eng, sub, wd in ((nc.gpsimd, on_g, 1), (nc.vector, on_v, gw)):
-                    for r, c0, c1 in runs(sub, wd):
-                        eng.tensor_tensor(
-                            h_bf[r][:, 512 * c0 : 512 * c1].rearrange("p (c x) -> p c x", x=512),
-                            sig[r][:, 512 * c0 : 512 * c1].rearrange("p (c x) -> p c x", x=512),
-                            ngain[:, r : r + 1].rearrange("p r j t -> p r (j t)").to_broadcast([P, c1 - c0, 512]),
-                            ALU.mult,
-                        )
-                for r, c0, c1 in runs(part, qw):
-                    if c1 - c0 == 3:
-                        pieces = [(c0, c0 + 2), (c0 + 2, c1)]
-                    else:
-                        pieces = [(c0, c1)]
-                    for d0, d1 in pieces:
-                        nc.vector.quantize_mx(
-                            out=h_q[r][:, JC * d0 : JC * d1].bitcast(FP8X4),
-                            scales=h_s[r][:, JC * d0 : JC * d1],
-                            in_=h_bf[r][:, 512 * d0 : 512 * d1],
-                        )
+        def outputs(half, slots):
+            lo = 512 * half
+            for i in range(2):
+                second_product([(q, lo + 256 * i, lo + 256 * i + 256) for q in range(2)], slots[i])
+            for q in range(2, 4):
+                second_product([(q, lo, lo + 512)], slots[q])
 
-            for part in (items[:early], items[early:]):
-                log_guard(part)
-                if early:
-                    gain_quant(part)
-            if not early:
-                gain_quant(items)
+        def first_product(r, chunks, slots, scalar_copies):
+            for c, slot in zip(chunks, slots):
+                banks[r, c] = psum.tile([P, 512], F32, name=f"a{r}{c}", tag=f"bank{slot}")
+                first_pass(r, c, 0)
+            for c in chunks:
+                first_pass(r, c, 1)
+                read_a(r, c, c in scalar_copies)
 
-        def second_product(g, q, pick):
-            lo, hi = GROUPS[g]
-            slot = free.pop(pick)
-            bank = psum.tile([P, 512], F32, name=f"y{g}{q}", tag=f"bank{slot}")
-            for c in range(lo, hi):
-                for r in range(2):
-                    nc.tensor.matmul_mx(
-                        out=bank[:, JC * (c - lo) : JC * (c - lo + 1)],
-                        lhsT=w4_t[:, r, 256 * q : 256 * q + 256].bitcast(FP4X4),
-                        lhsT_scale=w4_sc[:, r, 128 * q : 128 * q + 128],
-                        rhs=h_q[r][:, JC * c : JC * c + JC].bitcast(FP8X4),
-                        rhs_scale=h_s[r][:, JC * c : JC * c + JC],
-                        start=(r == 0),
-                        stop=(r == 1),
-                    )
-            nc.scalar.copy(y_sb[g, q][:], bank[:, 0 : JC * (hi - lo)])
-            free.append(slot)
-            if not TT:
-                nc.gpsimd.tensor_tensor(y_sb[g, q][:], y_sb[g, q][:], wgo_t[:, JC * lo : JC * hi], ALU.mult)
-
-        def scatter(g, q):
-            lo, hi = GROUPS[g]
-            dst = win[q][:].indirect(offs2_t[:, 8 * lo : 8 * hi])
-            if TT:
-                nc.vector.tensor_tensor(dst, y_sb[g, q][:], wgo_t[:, JC * lo : JC * hi], ALU.mult)
-            else:
-                nc.vector.tensor_copy(dst, y_sb[g, q][:])
-            if g == len(GROUPS) - 1:
-                nc.sync.dma_start(out=out[128 * q : 128 * q + 128, :], in_=win[q][:])
-
-        for step in PLAN:
-            if step[0] == "B":
-                batch(*step[1:])
-            elif step[0] == "Y":
-                second_product(step[1], step[2], step[3])
-            elif step[0] == "S":
-                scatter(step[1], step[2])
+        first_product(0, range(6), range(6), range(2))
+        first_product(1, range(4), [6, 7, 0, 1], [])
+        nc.vector.tensor_copy(v_s[1][:], tab_sc[:].indirect(offs_t[:, 48:64]))
+        gather(1, 6, 8)
+        eps_c = eps_after(1, 3)
+        finish_h(0, 0, eps_c, [2, 3])
+        finish_h(1, 0, eps_c, [4, 5])
+        finish_h(0, 1, eps_c, [6, 7])
+        finish_h(1, 1, eps_c, [0, 1])
+        finish_h(0, 2, eps_c, [2, 3])
+        for q in range(4):
+            (nc.gpsimd if q < 2 else nc.vector).memset(win[q][:].bitcast(I32), 0)
+        outputs(0, [0, 1, 2, 3])
+        first_product(1, [4, 5], [4, 5], [4, 5])
+        first_product(0, [6, 7], [6, 7], [6, 7])
+        first_product(1, [6, 7], [4, 5], [6, 7])
+        eps_c = eps_after(1, 7)
+        finish_h(1, 2, eps_c, [0, 1])
+        finish_h(0, 3, eps_c, [2, 3])
+        finish_h(1, 3, eps_c, [6, 7])
+        outputs(1, [2, 4, 5, 0])

@@ -23,6 +23,8 @@ JC = 128
 NJC = S // JC
 EPS = 2.0**-60
 LN2 = math.log(2.0)
+FLOOR = -20.0
+SCALAR_COLS = 192
 
 
 def tile_list_bond_softplus_store_kernel(
@@ -31,7 +33,6 @@ def tile_list_bond_softplus_store_kernel(
     nc = tc.nc
     with ExitStack() as ctx:
         keep = ctx.enter_context(tc.tile_pool(name="keep", bufs=1))
-        reuse = ctx.enter_context(tc.tile_pool(name="reuse", bufs=1))
         psum = ctx.enter_context(tc.psum_pool(name="psum", bufs=1))
 
         offs_t = keep.tile([P, S // 16], U16, name="offs_t")
@@ -40,46 +41,33 @@ def tile_list_bond_softplus_store_kernel(
         w4_sc = keep.tile([P, 2, N], U8, name="w4_sc", align_bytes=64)
         tab_w = [keep.tile([P, T], I32, name=f"tab_w{a}", align_bytes=64) for a in range(2)]
         ar = [(a, r) for r in range(2) for a in range(2)]
-        w_raw = {(0, r, 0): keep.tile([P, 4, 512], F32, name=f"w_raw0{r}") for r in range(2)}
-        for u in range(2):
-            w_raw[1, 0, u] = keep.tile([P, 4, 256], F32, name=f"w_raw10{u}")
-        w_raw[1, 1, 0] = keep.tile([P, 4, 256], F32, name="w_raw110")
-        w_raw[1, 1, 1] = keep.tile([P, 4, 256], F32, name="w_raw111")
-        w_bf = {k: keep.tile([P, 2048], BF16, name=f"w_bf{k[0]}{k[1]}", tag=f"bf{i}", align_bytes=64) for i, k in enumerate(ar[:3])}
-        w_bf[1, 1] = reuse.tile([P, 2048], BF16, name="w_bf11", offset=6144, align_bytes=64)
+        w_raw = {k: keep.tile([P, 4, 512], F32, name=f"w_raw{k[0]}{k[1]}") for k in ar}
+        w_bf = {k: keep.tile([P, 2048], BF16, name=f"w_bf{k[0]}{k[1]}", tag=f"bf{i}", align_bytes=64) for i, k in enumerate(ar)}
         w_q = {k: keep.tile([P, 512], U32, name=f"w_q{k[0]}{k[1]}", align_bytes=64) for k in ar}
         w_s = {k: keep.tile([P, 512], U8, name=f"w_s{k[0]}{k[1]}", align_bytes=64) for k in ar}
         w4_t = keep.tile([P, 2, 2 * N], U8, name="w4_t", align_bytes=64)
         wgo_t = keep.tile([P, S], F32, name="wgo_t")
         gain_t = keep.tile([P, 2, 4], F32, name="gain_t")
-        ngain = keep.tile([P, 2, JC, 4], F32, name="ngain")
-        cuts = [[(0, 8)], [(0, 2), (2, 6), (6, 8)]]
-        v_w = {(a, lo): keep.tile([P, JC * (hi - lo)], U32, name=f"v{a}{lo}", align_bytes=64) for a in range(2) for lo, hi in cuts[a][:2]}
-        v_w[1, 6] = reuse.tile([P, 2 * JC], U32, name="v16", offset=8192, align_bytes=64)
-        v_s = [
-            keep.tile([P, 6 * JC], U8, name="v_s0", align_bytes=64),
-            reuse.tile([P, 2 * JC], U8, name="v_s1", offset=9216, align_bytes=64),
-        ]
+        ngain = keep.tile([P, 2, 4], F32, name="ngain")
+        v_w = [keep.tile([P, S], U32, name=f"v{a}", align_bytes=64) for a in range(2)]
+        v_s = keep.tile([P, S], U8, name="v_s", align_bytes=64)
         rc = [(r, c) for r in range(2) for c in range(NJC)]
-        sig = {k: keep.tile([P, 512], F32, name=f"sig{k[0]}{k[1]}") for k in rc}
-        late = reuse.tile([P, 4, 512], F32, name="nega_late", offset=0, align_bytes=64)
-        nega = {
-            (r, c): late[:, c - 2] if r == 0 and 2 <= c < 6 else keep.tile([P, 512], F32, name=f"nega{r}{c}")[:]
+        sig_last = keep.tile([P, 2, 512], F32, name="sig_last")
+        sig = {
+            (r, c): sig_last[:, c // 4] if r == 1 and c % 4 == 3 else keep.tile([P, 512], F32, name=f"sig{r}{c}")[:]
             for r, c in rc
         }
+        nega = {k: keep.tile([P, 512], F32, name=f"nega{k[0]}{k[1]}") for k in rc}
         ident = keep.tile([P, P], F32, name="ident")
         h_q = {(r, half): keep.tile([P, 4 * JC], U32, name=f"h_q{r}{half}", align_bytes=64) for r in range(2) for half in range(2)}
         h_s = {(r, half): keep.tile([P, 4 * JC], U8, name=f"h_s{r}{half}", align_bytes=64) for r in range(2) for half in range(2)}
         win = [keep.tile([P, T2], F32, name=f"win{q}") for q in range(4)]
 
         def load_w(a, r):
-            wd = 512 // (a + 1)
-            for u in range(a + 1):
-                lo = 512 * r + wd * u
-                nc.sync.dma_start(
-                    out=w_raw[a, r, u][:],
-                    in_=w1[512 * a : 512 * a + 512, lo : lo + wd].rearrange("(p j) c -> p j c", j=4),
-                )
+            nc.sync.dma_start(
+                out=w_raw[a, r][:],
+                in_=w1[512 * a : 512 * a + 512, 512 * r : 512 * r + 512].rearrange("(p j) c -> p j c", j=4),
+            )
 
         def load_tab(a):
             nc.sync.dma_start(out=tab_w[a][:], in_=tab_words[a].rearrange("p t i -> p (t i)").bitcast(I32))
@@ -109,90 +97,123 @@ def tile_list_bond_softplus_store_kernel(
         nc.sync.dma_start(out=wgo_t[:], in_=wgo)
 
         def gather(a, lo, hi):
-            nc.vector.tensor_copy(v_w[a, lo][:], tab_w[a][:].bitcast(U32).indirect(offs_t[:, 8 * lo : 8 * hi]))
+            nc.vector.tensor_copy(v_w[a][:, JC * lo : JC * hi], tab_w[a][:].bitcast(U32).indirect(offs_t[:, 8 * lo : 8 * hi]))
 
-        def prep(a, r):
-            wd = 2048 // (a + 1)
-            for u in range(a + 1):
-                src = w_raw[a, r, u][:].rearrange("p j (m i) -> p m j i", i=4)
-                dst = w_bf[a, r][:, wd * u : wd * (u + 1)].rearrange("p (m i j) -> p m j i", i=4, j=4)
-                if r == 0 and u == 0:
-                    nc.scalar.copy(dst, src)
-                else:
-                    nc.vector.tensor_copy(dst, src)
+        def prep(a, r, scalar_cols):
+            for lo, hi, copy in ((0, scalar_cols, nc.scalar.copy), (scalar_cols, 512, nc.vector.tensor_copy)):
+                if hi > lo:
+                    copy(
+                        w_bf[a, r][:, 4 * lo : 4 * hi].rearrange("p (m i j) -> p m j i", i=4, j=4),
+                        w_raw[a, r][:, :, lo:hi].rearrange("p j (m i) -> p m j i", i=4),
+                    )
             nc.vector.quantize_mx(out=w_q[a, r][:].bitcast(FP8X4), scales=w_s[a, r][:], in_=w_bf[a, r][:])
 
         make_identity(nc, ident[:])
+        nc.gpsimd.tensor_scalar(ngain[:], gain_t[:], -1.0, 0.0, ALU.mult, ALU.add)
         gather(0, 0, 8)
-        nc.vector.tensor_copy(v_s[0][:], tab_sc[:].indirect(offs_t[:, 0:48]))
-        prep(0, 0)
-        prep(1, 0)
+        nc.vector.tensor_copy(v_s[:], tab_sc[:].indirect(offs_t[:]))
+        prep(0, 0, 512)
+        prep(1, 0, SCALAR_COLS)
         gather(1, 0, 2)
-        gather(1, 2, 6)
-        prep(0, 1)
-        prep(1, 1)
-        nc.scalar.activation(ngain[:], gain_t[:].unsqueeze(2).to_broadcast([P, 2, JC, 4]), ACT.Copy, scale=-1.0)
+        gather(1, 2, 8)
+        prep(0, 1, 0)
+        prep(1, 1, 0)
 
         banks = {}
 
         def first_pass(r, c, a):
-            lo = max(x for x, y in cuts[a] if x <= c)
+            cols = slice(JC * c, JC * (c + 1))
             nc.tensor.matmul_mx(
                 out=banks[r, c][:],
-                lhsT=v_w[a, lo][:, JC * (c - lo) : JC * (c - lo + 1)].bitcast(FP8X4),
-                lhsT_scale=v_s[c // 6][4 * a : 128, JC * (c % 6) : JC * (c % 6 + 1)],
+                lhsT=v_w[a][:, cols].bitcast(FP8X4),
+                lhsT_scale=v_s[4 * a : 128, cols],
                 rhs=w_q[a, r][:].bitcast(FP8X4),
                 rhs_scale=w_s[a, r][:],
                 start=(a == 0),
                 stop=(a == 1),
             )
 
-        def read_a(r, c, copy_on_scalar):
-            by_t = banks[r, c][:].rearrange("p (m t) -> p t m", t=4)
-            nc.scalar.activation(sig[r, c][:].rearrange("p (t m) -> p t m", t=4), by_t, ACT.Sigmoid)
-            dst = nega[r, c].rearrange("p (t m) -> p t m", t=4)
-            if copy_on_scalar:
-                nc.scalar.activation(dst, by_t, ACT.Copy, scale=-1.0)
-            else:
-                nc.vector.tensor_scalar(dst, by_t, -1.0, None, ALU.mult)
+        def by_t(r, c):
+            return banks[r, c][:].rearrange("p (m t) -> p t m", t=4)
 
-        def eps_after(r, c):
-            eps_c = keep.tile([P, 1], F32, name=f"eps{r}{c}")
-            nc.scalar.activation(eps_c[:], sig[r, c][:, 511:512], ACT.Copy, scale=0.0, bias=EPS)
-            return eps_c
+        def product(r, c, slot):
+            banks[r, c] = psum.tile([P, 512], F32, name=f"a{r}{c}", tag=f"bank{slot}")
+            first_pass(r, c, 0)
+            first_pass(r, c, 1)
 
-        def turn(u, src, first):
-            for t in range(4):
-                nc.tensor.matmul(
-                    u[:, t, :], src[:, 128 * t : 128 * t + 128], ident[:],
-                    start=(first and t == 0), stop=(not first and t == 3), is_transpose=True,
-                )
+        def sigmoid_from_bank(r, c):
+            nc.scalar.activation(sig[r, c].rearrange("p (t m) -> p t m", t=4), by_t(r, c), ACT.Sigmoid)
 
-        def finish_h(r, g, eps_c, slots):
-            h_bf = keep.tile([P, 2048], BF16, name=f"h_bf{r}{g}", tag=f"bf{g}", align_bytes=64)
-            for i in range(2):
-                c = 2 * g + i
-                u = psum.tile([P, 4, JC], F32, name=f"u{r}{c}", tag=f"bank{slots[i]}")
-                turn(u, nega[r, c], True)
-                nc.scalar.activation(sig[r, c][:], sig[r, c][:], ACT.Ln, bias=eps_c[:], scale=2.0)
-                turn(u, sig[r, c], False)
-                nc.vector.scalar_tensor_tensor(
-                    h_bf[:, 512 * i : 512 * i + 512].rearrange("p (j t) -> p j t", t=4),
-                    u[:].rearrange("p t j -> p j t"),
-                    LN2,
-                    ngain[:, r],
-                    ALU.min,
-                    ALU.mult,
-                )
+        def copy_on_scalar(r, c):
+            nc.scalar.activation(nega[r, c][:].rearrange("p (t m) -> p t m", t=4), by_t(r, c), ACT.Copy, scale=-1.0)
+
+        def copy_on_vector(r, c):
+            nc.vector.tensor_scalar(nega[r, c][:].rearrange("p (t m) -> p t m", t=4), by_t(r, c), -1.0, None, ALU.mult)
+
+        def floored_copy_then_sigmoid(r, c):
+            dst = nega[r, c][:].rearrange("p (t m) -> p t m", t=4)
+            nc.vector.tensor_scalar(dst, by_t(r, c), FLOOR, -1.0, ALU.max, ALU.mult)
+            nc.scalar.activation(sig[r, c], nega[r, c][:], ACT.Sigmoid, scale=-1.0)
+
+        def turn(dst, src, t, start, stop):
+            nc.tensor.matmul(dst, src[:, 128 * t : 128 * t + 128], ident[:], start=start, stop=stop, is_transpose=True)
+
+        def log_of(r, c):
+            nc.scalar.activation(sig[r, c], sig[r, c], ACT.Ln, bias=eps_c[:, 0:1], scale=2.0)
+
+        h_bf = {}
+
+        def h_tile(r, g):
+            h_bf[r, g] = keep.tile([P, 2048], BF16, name=f"h_bf{r}{g}", tag=f"bf{(2 * g + r) % 4}", align_bytes=64)
+            return h_bf[r, g]
+
+        def quantise_h(r, g):
             cols = slice(2 * JC * (g % 2), 2 * JC * (g % 2 + 1))
             nc.vector.quantize_mx(
-                out=h_q[r, g // 2][:, cols].bitcast(FP8X4), scales=h_s[r, g // 2][:, cols], in_=h_bf[:, 0:1024]
+                out=h_q[r, g // 2][:, cols].bitcast(FP8X4), scales=h_s[r, g // 2][:, cols], in_=h_bf[r, g][:, 0:1024]
             )
+
+        def finish_on_vector(r, c, slot):
+            i = c % 2
+            dst = h_tile(r, c // 2) if i == 0 else h_bf[r, c // 2]
+            u = psum.tile([P, 4, JC], F32, name=f"u{r}{c}", tag=f"bank{slot}")
+            for t in range(4):
+                turn(u[:, t, :], nega[r, c], t, t == 0, False)
+            log_of(r, c)
+            for t in range(4):
+                turn(u[:, t, :], sig[r, c], t, False, t == 3)
+            nc.vector.scalar_tensor_tensor(
+                dst[:, 512 * i : 512 * i + 512].rearrange("p (j t) -> p j t", t=4),
+                u[:].rearrange("p t j -> p j t"),
+                LN2,
+                ngain[:, r].unsqueeze(1).to_broadcast([P, JC, 4]),
+                ALU.min,
+                ALU.mult,
+            )
+
+        def finish_on_scalar(r, g, slots):
+            dst = h_tile(r, g)
+            u = [psum.tile([P, 2, 2 * JC], F32, name=f"u{r}{g}{b}", tag=f"bank{slots[b]}") for b in range(2)]
+            for i in range(2):
+                for t in range(4):
+                    turn(u[t // 2][:, t % 2, JC * i : JC * (i + 1)], nega[r, 2 * g + i], t, i == 0 and t % 2 == 0, False)
+            for i in range(2):
+                for t in range(4):
+                    turn(u[t // 2][:, t % 2, JC * i : JC * (i + 1)], sig[r, 2 * g + i], t, False, i == 1 and t % 2 == 1)
+            by_t = keep.tile([P, 4, 2 * JC], BF16, name=f"by_t{r}{g}")
+            for t in range(4):
+                nc.scalar.activation(by_t[:, t, :], u[t // 2][:, t % 2, :], ACT.Copy, scale=ngain[:, r, t : t + 1])
+            nc.scalar.copy(
+                dst[:, 0:1024].rearrange("p (c i t) -> p c t i", i=4, t=4),
+                by_t[:].rearrange("p t (c i) -> p c t i", i=4),
+            )
+            quantise_h(r, g)
 
         def second_product(parts, slot):
             name = "y" + "".join(f"{q}{lo}" for q, lo, hi in parts)
+            width = sum(hi - lo for q, lo, hi in parts)
             bank = psum.tile([P, 512], F32, name=name, tag=f"bank{slot}")
-            wd = 512 if len(parts) == 1 else JC
+            wd = 512 if parts[0][2] - parts[0][1] == 512 else JC
             at = 0
             for q, lo, hi in parts:
                 for c0 in range(lo, hi, wd):
@@ -208,8 +229,8 @@ def tile_list_bond_softplus_store_kernel(
                             stop=(r == 1),
                         )
                     at += wd
-            y = keep.tile([P, 512], F32, name="s" + name)
-            nc.scalar.copy(y[:], bank[:])
+            y = keep.tile([P, width], F32, name="s" + name)
+            nc.scalar.copy(y[:], bank[:, 0:width])
             at = 0
             for q, lo, hi in parts:
                 nc.vector.tensor_tensor(
@@ -219,39 +240,51 @@ def tile_list_bond_softplus_store_kernel(
                 if hi == S:
                     nc.sync.dma_start(out=out[128 * q : 128 * q + 128, :], in_=win[q][:])
 
-        def outputs(half, slots):
-            lo = 512 * half
-            for i in range(2):
-                second_product([(q, lo + 256 * i, lo + 256 * i + 256) for q in range(2)], slots[i])
-            for q in range(2, 4):
-                second_product([(q, lo, lo + 512)], slots[q])
-
-        def first_product(r, chunks, slots, scalar_copies):
-            for c, slot in zip(chunks, slots):
-                banks[r, c] = psum.tile([P, 512], F32, name=f"a{r}{c}", tag=f"bank{slot}")
-                first_pass(r, c, 0)
-            for c in chunks:
-                first_pass(r, c, 1)
-                read_a(r, c, c in scalar_copies)
-
-        first_product(0, range(6), range(6), range(2))
-        first_product(1, range(4), [6, 7, 0, 1], [])
-        nc.vector.tensor_copy(v_s[1][:], tab_sc[:].indirect(offs_t[:, 48:64]))
-        gather(1, 6, 8)
-        eps_c = eps_after(1, 3)
-        finish_h(0, 0, eps_c, [2, 3])
-        finish_h(1, 0, eps_c, [4, 5])
-        finish_h(0, 1, eps_c, [6, 7])
-        finish_h(1, 1, eps_c, [0, 1])
-        finish_h(0, 2, eps_c, [2, 3])
+        for c in range(4):
+            product(0, c, c)
+            sigmoid_from_bank(0, c)
+            if c < 3:
+                copy_on_scalar(0, c)
+        for r in range(2):
+            for c in range(4, 8):
+                product(r, c, c)
+                floored_copy_then_sigmoid(r, c)
+        for c, slot in enumerate([0, 1, 2, 4]):
+            product(1, c, slot)
+            sigmoid_from_bank(1, c)
+        copy_on_vector(0, 3)
+        for c in range(4):
+            copy_on_vector(1, c)
+        eps_c = keep.tile([P, 2], F32, name="eps_c")
+        nc.scalar.activation(eps_c[:], sig_last[:, :, 511], ACT.Copy, scale=0.0, bias=EPS)
         for q in range(4):
             (nc.gpsimd if q < 2 else nc.vector).memset(win[q][:].bitcast(I32), 0)
-        outputs(0, [0, 1, 2, 3])
-        first_product(1, [4, 5], [4, 5], [4, 5])
-        first_product(0, [6, 7], [6, 7], [6, 7])
-        first_product(1, [6, 7], [4, 5], [6, 7])
-        eps_c = eps_after(1, 7)
-        finish_h(1, 2, eps_c, [0, 1])
-        finish_h(0, 3, eps_c, [2, 3])
-        finish_h(1, 3, eps_c, [6, 7])
-        outputs(1, [2, 4, 5, 0])
+
+        finish_on_vector(0, 0, 5)
+        finish_on_vector(0, 1, 6)
+        finish_on_vector(1, 0, 7)
+        quantise_h(0, 0)
+        finish_on_vector(1, 1, 3)
+        finish_on_vector(0, 2, 0)
+        quantise_h(1, 0)
+        finish_on_vector(0, 3, 1)
+        finish_on_vector(1, 2, 2)
+        quantise_h(0, 1)
+        finish_on_vector(1, 3, 4)
+        quantise_h(1, 1)
+        second_product([(0, 0, 256), (1, 0, 256)], 5)
+        second_product([(0, 256, 512), (1, 256, 512)], 6)
+        second_product([(2, 0, 512)], 7)
+        for c in range(4, 8):
+            log_of(0, c)
+            log_of(1, c)
+        finish_on_scalar(0, 2, [3, 0])
+        finish_on_scalar(1, 2, [1, 2])
+        second_product([(3, 0, 512)], 2)
+        finish_on_scalar(0, 3, [4, 5])
+        second_product([(0, 512, 768)], 5)
+        finish_on_scalar(1, 3, [6, 7])
+        second_product([(1, 512, 768)], 7)
+        second_product([(0, 768, 1024), (1, 768, 1024)], 3)
+        second_product([(2, 512, 1024)], 0)
+        second_product([(3, 512, 1024)], 1)

@@ -24,7 +24,6 @@ NJC = S // JC
 EPS = 2.0**-60
 LN2 = math.log(2.0)
 FLOOR = -20.0
-SCALAR_COLS = 192
 
 
 def tile_list_bond_softplus_store_kernel(
@@ -33,6 +32,7 @@ def tile_list_bond_softplus_store_kernel(
     nc = tc.nc
     with ExitStack() as ctx:
         keep = ctx.enter_context(tc.tile_pool(name="keep", bufs=1))
+        reuse = ctx.enter_context(tc.tile_pool(name="reuse", bufs=1))
         psum = ctx.enter_context(tc.psum_pool(name="psum", bufs=1))
 
         offs_t = keep.tile([P, S // 16], U16, name="offs_t")
@@ -40,53 +40,61 @@ def tile_list_bond_softplus_store_kernel(
         tab_sc = keep.tile([P, T], U8, name="tab_sc", align_bytes=64)
         w4_sc = keep.tile([P, 2, N], U8, name="w4_sc", align_bytes=64)
         tab_w = [keep.tile([P, T], I32, name=f"tab_w{a}", align_bytes=64) for a in range(2)]
-        ar = [(a, r) for r in range(2) for a in range(2)]
-        w_raw = {k: keep.tile([P, 4, 512], F32, name=f"w_raw{k[0]}{k[1]}") for k in ar}
-        w_bf = {k: keep.tile([P, 2048], BF16, name=f"w_bf{k[0]}{k[1]}", tag=f"bf{i}", align_bytes=64) for i, k in enumerate(ar)}
-        w_q = {k: keep.tile([P, 512], U32, name=f"w_q{k[0]}{k[1]}", align_bytes=64) for k in ar}
-        w_s = {k: keep.tile([P, 512], U8, name=f"w_s{k[0]}{k[1]}", align_bytes=64) for k in ar}
+        w_raw = {(a, k): keep.tile([P, 4, 256], F32, name=f"w_raw{a}{k}") for k in range(2) for a in range(2)}
+        for k in range(2, 4):
+            for a in range(2):
+                w_raw[a, k] = reuse.tile([P, 4, 256], F32, name=f"w_raw{a}{k}", offset=4096 * (2 * k + a - 4), align_bytes=64)
+        w_bf = [reuse.tile([P, 2048], BF16, name="w_bf0", offset=16384, align_bytes=64)]
+        w_bf = w_bf + [keep.tile([P, 2048], BF16, name=f"w_bf{k}", align_bytes=64) for k in range(1, 4)]
+        w_q = [keep.tile([P, 512], U32, name=f"w_q{k}", align_bytes=64) for k in range(4)]
+        w_s = [keep.tile([P, 512], U8, name=f"w_s{k}", align_bytes=64) for k in range(4)]
         w4_t = keep.tile([P, 2, 2 * N], U8, name="w4_t", align_bytes=64)
         wgo_t = keep.tile([P, S], F32, name="wgo_t")
         gain_t = keep.tile([P, 2, 4], F32, name="gain_t")
         ngain = keep.tile([P, 2, 4], F32, name="ngain")
-        v_w = [keep.tile([P, S], U32, name=f"v{a}", align_bytes=64) for a in range(2)]
+        v_w = [keep.tile([P, S], U32, name="v0", align_bytes=64), reuse.tile([P, S], U32, name="v1", offset=16384, align_bytes=64)]
         v_s = keep.tile([P, S], U8, name="v_s", align_bytes=64)
+        sig_late = keep.tile([P, 4, 1024], F32, name="sig_late")
+        sig2 = {(1, g): sig_late[:, g] for g in range(4)}
+        for g in range(4):
+            sig2[0, g] = keep.tile([P, 1024], F32, name=f"sig0{g}")[:]
+        nega2 = {(r, g): keep.tile([P, 1024], F32, name=f"nega{r}{g}")[:] for r in range(2) for g in range(2)}
+        for r in range(2):
+            for g in range(2, 4):
+                nega2[r, g] = reuse.tile([P, 1024], F32, name=f"nega{r}{g}", offset=4096 * (2 * r + g - 2), align_bytes=64)[:]
+        minus = keep.tile([P, 1], F32, name="minus")
         rc = [(r, c) for r in range(2) for c in range(NJC)]
-        sig_last = keep.tile([P, 2, 512], F32, name="sig_last")
-        sig = {
-            (r, c): sig_last[:, c // 4] if r == 1 and c % 4 == 3 else keep.tile([P, 512], F32, name=f"sig{r}{c}")[:]
-            for r, c in rc
-        }
-        nega = {k: keep.tile([P, 512], F32, name=f"nega{k[0]}{k[1]}") for k in rc}
+        sig = {(r, c): sig2[r, c // 2][:, 512 * (c % 2) : 512 * (c % 2 + 1)] for r, c in rc}
+        nega = {(r, c): nega2[r, c // 2][:, 512 * (c % 2) : 512 * (c % 2 + 1)] for r, c in rc}
         ident = keep.tile([P, P], F32, name="ident")
         h_q = {(r, half): keep.tile([P, 4 * JC], U32, name=f"h_q{r}{half}", align_bytes=64) for r in range(2) for half in range(2)}
         h_s = {(r, half): keep.tile([P, 4 * JC], U8, name=f"h_s{r}{half}", align_bytes=64) for r in range(2) for half in range(2)}
         win = [keep.tile([P, T2], F32, name=f"win{q}") for q in range(4)]
 
-        def load_w(a, r):
-            nc.sync.dma_start(
-                out=w_raw[a, r][:],
-                in_=w1[512 * a : 512 * a + 512, 512 * r : 512 * r + 512].rearrange("(p j) c -> p j c", j=4),
-            )
+        def load_w(k):
+            for a in range(2):
+                nc.sync.dma_start(
+                    out=w_raw[a, k][:],
+                    in_=w1[512 * a : 512 * a + 512, 256 * k : 256 * k + 256].rearrange("(p j) c -> p j c", j=4),
+                )
 
         def load_tab(a):
             nc.sync.dma_start(out=tab_w[a][:], in_=tab_words[a].rearrange("p t i -> p (t i)").bitcast(I32))
 
-        nc.vector.memset(tab_sc[:].bitcast(I32), 0)
+        nc.gpsimd.memset(tab_sc[:].bitcast(I32), 0)
         nc.sync.dma_start(offs_t[:], offs)
         nc.sync.dma_start(offs2_t[:], offs2)
-        nc.sync.dma_start(out=gain_t[:], in_=gain.rearrange("(a p t) -> p a t", a=2, t=4))
         load_tab(0)
         for qd in range(4):
             nc.sync.dma_start(
                 out=tab_sc[32 * qd : 32 * qd + 8, :].bitcast(I32),
                 in_=tab_scales[:, 4 * qd : 4 * qd + 4, :].bitcast(I32),
             )
-        load_w(0, 0)
-        load_w(1, 0)
+        load_w(0)
         load_tab(1)
-        load_w(0, 1)
-        load_w(1, 1)
+        for k in range(1, 4):
+            load_w(k)
+        nc.sync.dma_start(out=gain_t[:], in_=gain.rearrange("(a p t) -> p a t", a=2, t=4))
         nc.vector.memset(w4_sc[:].rearrange("p a n -> p (a n)").bitcast(I32), 0)
         for qd in range(4):
             nc.sync.dma_start(
@@ -97,74 +105,72 @@ def tile_list_bond_softplus_store_kernel(
         nc.sync.dma_start(out=wgo_t[:], in_=wgo)
 
         def gather(a, lo, hi):
-            nc.vector.tensor_copy(v_w[a][:, JC * lo : JC * hi], tab_w[a][:].bitcast(U32).indirect(offs_t[:, 8 * lo : 8 * hi]))
+            nc.vector.tensor_copy(v_w[a][:, 256 * lo : 256 * hi], tab_w[a][:].bitcast(U32).indirect(offs_t[:, 16 * lo : 16 * hi]))
 
-        def prep(a, r, scalar_cols):
-            for lo, hi, copy in ((0, scalar_cols, nc.scalar.copy), (scalar_cols, 512, nc.vector.tensor_copy)):
-                if hi > lo:
-                    copy(
-                        w_bf[a, r][:, 4 * lo : 4 * hi].rearrange("p (m i j) -> p m j i", i=4, j=4),
-                        w_raw[a, r][:, :, lo:hi].rearrange("p j (m i) -> p m j i", i=4),
-                    )
-            nc.vector.quantize_mx(out=w_q[a, r][:].bitcast(FP8X4), scales=w_s[a, r][:], in_=w_bf[a, r][:])
+        def gather_scales(lo, hi):
+            nc.vector.tensor_copy(v_s[:, 256 * lo : 256 * hi], tab_sc[:].indirect(offs_t[:, 16 * lo : 16 * hi]))
 
-        make_identity(nc, ident[:])
-        nc.gpsimd.tensor_scalar(ngain[:], gain_t[:], -1.0, 0.0, ALU.mult, ALU.add)
-        gather(0, 0, 8)
-        nc.vector.tensor_copy(v_s[:], tab_sc[:].indirect(offs_t[:]))
-        prep(0, 0, 512)
-        prep(1, 0, SCALAR_COLS)
-        gather(1, 0, 2)
-        gather(1, 2, 8)
-        prep(0, 1, 0)
-        prep(1, 1, 0)
+        def cast(a, k, copy):
+            copy(
+                w_bf[k][:, 1024 * a : 1024 * a + 1024].rearrange("p (m i j) -> p m j i", i=4, j=4),
+                w_raw[a, k][:].rearrange("p j (m i) -> p m j i", i=4),
+            )
+
+        def quantise_w(k, lo, hi):
+            cols = slice(256 * lo, 256 * hi)
+            nc.vector.quantize_mx(out=w_q[k][:, cols].bitcast(FP8X4), scales=w_s[k][:, cols], in_=w_bf[k][:, 1024 * lo : 1024 * hi])
 
         banks = {}
 
-        def first_pass(r, c, a):
-            cols = slice(JC * c, JC * (c + 1))
-            nc.tensor.matmul_mx(
-                out=banks[r, c][:],
-                lhsT=v_w[a][:, cols].bitcast(FP8X4),
-                lhsT_scale=v_s[4 * a : 128, cols],
-                rhs=w_q[a, r][:].bitcast(FP8X4),
-                rhs_scale=w_s[a, r][:],
-                start=(a == 0),
-                stop=(a == 1),
-            )
+        def product(k, g, slot):
+            banks[k, g] = psum.tile([P, 2, 256], F32, name=f"a{k}{g}", tag=f"bank{slot}")
+            for a in range(2):
+                for i in range(2):
+                    cols = slice(JC * (2 * g + i), JC * (2 * g + i + 1))
+                    nc.tensor.matmul_mx(
+                        out=banks[k, g][:, i, :],
+                        lhsT=v_w[a][:, cols].bitcast(FP8X4),
+                        lhsT_scale=v_s[4 * a : 128, cols],
+                        rhs=w_q[k][:, 256 * a : 256 * a + 256].bitcast(FP8X4),
+                        rhs_scale=w_s[k][:, 256 * a : 256 * a + 256],
+                        start=(a == 0 and i == 0),
+                        stop=(a == 1 and i == 1),
+                    )
 
-        def by_t(r, c):
-            return banks[r, c][:].rearrange("p (m t) -> p t m", t=4)
+        def from_bank(k, g):
+            return banks[k, g][:].rearrange("p i (m t) -> p i t m", t=4)
 
-        def product(r, c, slot):
-            banks[r, c] = psum.tile([P, 512], F32, name=f"a{r}{c}", tag=f"bank{slot}")
-            first_pass(r, c, 0)
-            first_pass(r, c, 1)
+        def share(pair, k):
+            return pair.rearrange("p (i t m) -> p i t m", i=2, t=4)[:, :, :, 64 * (k % 2) : 64 * (k % 2) + 64]
 
-        def sigmoid_from_bank(r, c):
-            nc.scalar.activation(sig[r, c].rearrange("p (t m) -> p t m", t=4), by_t(r, c), ACT.Sigmoid)
+        def sigmoid_from_bank(k, g):
+            nc.scalar.activation(share(sig2[k // 2, g], k), from_bank(k, g), ACT.Sigmoid)
 
-        def copy_on_scalar(r, c):
-            nc.scalar.activation(nega[r, c][:].rearrange("p (t m) -> p t m", t=4), by_t(r, c), ACT.Copy, scale=-1.0)
+        def copy_on_scalar(k, g):
+            nc.scalar.activation(share(nega2[k // 2, g], k), from_bank(k, g), ACT.Copy, scale=-1.0)
 
-        def copy_on_vector(r, c):
-            nc.vector.tensor_scalar(nega[r, c][:].rearrange("p (t m) -> p t m", t=4), by_t(r, c), -1.0, None, ALU.mult)
+        def copy_on_vector(k, g, factor):
+            nc.vector.tensor_scalar(share(nega2[k // 2, g], k), from_bank(k, g), factor, None, ALU.mult)
 
-        def floored_copy_then_sigmoid(r, c):
-            dst = nega[r, c][:].rearrange("p (t m) -> p t m", t=4)
-            nc.vector.tensor_scalar(dst, by_t(r, c), FLOOR, -1.0, ALU.max, ALU.mult)
-            nc.scalar.activation(sig[r, c], nega[r, c][:], ACT.Sigmoid, scale=-1.0)
+        def floored_copy_then_sigmoid(k, g):
+            dst = share(nega2[k // 2, g], k)
+            nc.vector.tensor_scalar(dst, from_bank(k, g), FLOOR, -1.0, ALU.max, ALU.mult)
+            nc.scalar.activation(share(sig2[k // 2, g], k), dst, ACT.Sigmoid, scale=-1.0)
 
         def turn(dst, src, t, start, stop):
             nc.tensor.matmul(dst, src[:, 128 * t : 128 * t + 128], ident[:], start=start, stop=stop, is_transpose=True)
 
-        def log_of(r, c):
-            nc.scalar.activation(sig[r, c], sig[r, c], ACT.Ln, bias=eps_c[:, 0:1], scale=2.0)
+        def log_of(x):
+            nc.scalar.activation(x, x, ACT.Ln, bias=eps_c[:, 0:1], scale=2.0)
+
+        def second_product(parts, slot):
+            place(*multiply(parts, slot))
 
         h_bf = {}
+        ys = []
 
         def h_tile(r, g):
-            h_bf[r, g] = keep.tile([P, 2048], BF16, name=f"h_bf{r}{g}", tag=f"bf{(2 * g + r) % 4}", align_bytes=64)
+            h_bf[r, g] = keep.tile([P, 1024], BF16, name=f"h_bf{r}{g}", align_bytes=64)
             return h_bf[r, g]
 
         def quantise_h(r, g):
@@ -179,7 +185,7 @@ def tile_list_bond_softplus_store_kernel(
             u = psum.tile([P, 4, JC], F32, name=f"u{r}{c}", tag=f"bank{slot}")
             for t in range(4):
                 turn(u[:, t, :], nega[r, c], t, t == 0, False)
-            log_of(r, c)
+            log_of(sig[r, c])
             for t in range(4):
                 turn(u[:, t, :], sig[r, c], t, False, t == 3)
             nc.vector.scalar_tensor_tensor(
@@ -209,7 +215,7 @@ def tile_list_bond_softplus_store_kernel(
             )
             quantise_h(r, g)
 
-        def second_product(parts, slot):
+        def multiply(parts, slot):
             name = "y" + "".join(f"{q}{lo}" for q, lo, hi in parts)
             width = sum(hi - lo for q, lo, hi in parts)
             bank = psum.tile([P, 512], F32, name=name, tag=f"bank{slot}")
@@ -229,8 +235,12 @@ def tile_list_bond_softplus_store_kernel(
                             stop=(r == 1),
                         )
                     at += wd
+            return parts, bank, name, width
+
+        def place(parts, bank, name, width):
             y = keep.tile([P, width], F32, name="s" + name)
             nc.scalar.copy(y[:], bank[:, 0:width])
+            ys.append(y)
             at = 0
             for q, lo, hi in parts:
                 nc.vector.tensor_tensor(
@@ -240,51 +250,83 @@ def tile_list_bond_softplus_store_kernel(
                 if hi == S:
                     nc.sync.dma_start(out=out[128 * q : 128 * q + 128, :], in_=win[q][:])
 
-        for c in range(4):
-            product(0, c, c)
-            sigmoid_from_bank(0, c)
-            if c < 3:
-                copy_on_scalar(0, c)
-        for r in range(2):
-            for c in range(4, 8):
-                product(r, c, c)
-                floored_copy_then_sigmoid(r, c)
-        for c, slot in enumerate([0, 1, 2, 4]):
-            product(1, c, slot)
-            sigmoid_from_bank(1, c)
-        copy_on_vector(0, 3)
-        for c in range(4):
-            copy_on_vector(1, c)
-        eps_c = keep.tile([P, 2], F32, name="eps_c")
-        nc.scalar.activation(eps_c[:], sig_last[:, :, 511], ACT.Copy, scale=0.0, bias=EPS)
+        make_identity(nc, ident[:])
+        gather(0, 0, 4)
+        gather_scales(0, 4)
+        cast(0, 0, nc.scalar.copy)
+        cast(1, 0, nc.scalar.copy)
+        quantise_w(0, 0, 2)
+        gather(1, 0, 1)
+        gather(1, 1, 2)
+        cast(0, 1, nc.vector.tensor_copy)
+        cast(1, 1, nc.vector.tensor_copy)
+        quantise_w(1, 0, 2)
+        gather(1, 2, 4)
+        for k in range(2, 4):
+            cast(0, k, nc.scalar.copy)
+            if k == 3:
+                quantise_w(k, 0, 1)
+            cast(1, k, nc.vector.tensor_copy)
+            quantise_w(k, k - 2, 2)
+
+        for g in range(2):
+            product(0, g, g)
+            sigmoid_from_bank(0, g)
+            if g == 0:
+                copy_on_scalar(0, g)
+            else:
+                copy_on_vector(0, g, -1.0)
+        for g in range(2, 4):
+            product(0, g, g)
+            floored_copy_then_sigmoid(0, g)
+        for g in range(2):
+            product(1, g, 4 + g)
+            sigmoid_from_bank(1, g)
+        for g in range(2, 4):
+            product(1, g, 4 + g)
+            floored_copy_then_sigmoid(1, g)
+        for k, slots in ((2, [0, 1, 2, 3]), (3, [6, 7, 2, 3])):
+            for g in range(2):
+                product(k, g + 2, slots[g + 2])
+                product(k, g, slots[g])
+                sigmoid_from_bank(k, g)
+                floored_copy_then_sigmoid(k, g + 2)
+        nc.gpsimd.tensor_scalar(ngain[:], gain_t[:], -1.0, 0.0, ALU.mult, ALU.add)
+        nc.gpsimd.tensor_scalar(minus[:], nega2[1, 3][:, 0:1], 0.0, -1.0, ALU.mult, ALU.add)
+        for g in range(2):
+            for k in range(1, 4):
+                copy_on_vector(k, g, minus[:, 0:1])
+        eps_c = keep.tile([P, 4], F32, name="eps_c")
+        nc.scalar.activation(eps_c[:], sig_late[:, :, 1023], ACT.Copy, scale=0.0, bias=EPS)
         for q in range(4):
             (nc.gpsimd if q < 2 else nc.vector).memset(win[q][:].bitcast(I32), 0)
 
-        finish_on_vector(0, 0, 5)
-        finish_on_vector(0, 1, 6)
-        finish_on_vector(1, 0, 7)
+        finish_on_vector(0, 0, 2)
+        finish_on_vector(0, 1, 3)
+        finish_on_vector(1, 0, 4)
+        finish_on_vector(1, 1, 0)
         quantise_h(0, 0)
-        finish_on_vector(1, 1, 3)
-        finish_on_vector(0, 2, 0)
         quantise_h(1, 0)
-        finish_on_vector(0, 3, 1)
-        finish_on_vector(1, 2, 2)
+        first = multiply([(0, 0, 256), (1, 0, 256)], 2)
+        finish_on_vector(0, 2, 6)
+        finish_on_vector(0, 3, 5)
+        finish_on_vector(1, 2, 1)
+        finish_on_vector(1, 3, 7)
         quantise_h(0, 1)
-        finish_on_vector(1, 3, 4)
         quantise_h(1, 1)
-        second_product([(0, 0, 256), (1, 0, 256)], 5)
-        second_product([(0, 256, 512), (1, 256, 512)], 6)
-        second_product([(2, 0, 512)], 7)
-        for c in range(4, 8):
-            log_of(0, c)
-            log_of(1, c)
-        finish_on_scalar(0, 2, [3, 0])
-        finish_on_scalar(1, 2, [1, 2])
-        second_product([(3, 0, 512)], 2)
-        finish_on_scalar(0, 3, [4, 5])
-        second_product([(0, 512, 768)], 5)
-        finish_on_scalar(1, 3, [6, 7])
-        second_product([(1, 512, 768)], 7)
-        second_product([(0, 768, 1024), (1, 768, 1024)], 3)
-        second_product([(2, 512, 1024)], 0)
-        second_product([(3, 512, 1024)], 1)
+        place(*first)
+        second_product([(0, 256, 512), (1, 256, 512)], 3)
+        second_product([(2, 0, 512)], 4)
+        for g in range(2, 4):
+            log_of(sig2[0, g])
+            log_of(sig2[1, g])
+        finish_on_scalar(0, 2, [0, 6])
+        finish_on_scalar(1, 2, [5, 1])
+        second_product([(3, 0, 512)], 1)
+        finish_on_scalar(0, 3, [7, 2])
+        second_product([(0, 512, 768)], 2)
+        finish_on_scalar(1, 3, [3, 4])
+        second_product([(1, 512, 768)], 4)
+        second_product([(0, 768, 1024), (1, 768, 1024)], 0)
+        second_product([(2, 512, 1024)], 6)
+        second_product([(3, 512, 1024)], 5)

@@ -46,13 +46,13 @@ def tile_list_bond_softplus_store_kernel(
                 w_raw[a, k] = reuse.tile([P, 4, 256], F32, name=f"w_raw{a}{k}", offset=4096 * (2 * k + a - 4), align_bytes=64)
         w_bf = [reuse.tile([P, 2048], BF16, name="w_bf0", offset=16384, align_bytes=64)]
         w_bf = w_bf + [keep.tile([P, 2048], BF16, name=f"w_bf{k}", align_bytes=64) for k in range(1, 4)]
-        w_q = [keep.tile([P, 512], U32, name=f"w_q{k}", align_bytes=64) for k in range(4)]
+        w_q = [reuse.tile([P, 512], U32, name=f"w_q{k}", offset=24576 + 2048 * k, align_bytes=64) for k in range(4)]
         w_s = [keep.tile([P, 512], U8, name=f"w_s{k}", align_bytes=64) for k in range(4)]
         w4_t = keep.tile([P, 2, 2 * N], U8, name="w4_t", align_bytes=64)
         wgo_t = keep.tile([P, S], F32, name="wgo_t")
         gain_t = keep.tile([P, 2, 4], F32, name="gain_t")
         ngain = keep.tile([P, 2, 4], F32, name="ngain")
-        v_w = [keep.tile([P, S], U32, name="v0", align_bytes=64), reuse.tile([P, S], U32, name="v1", offset=16384, align_bytes=64)]
+        v_w = [reuse.tile([P, S], U32, name="v0", offset=20480, align_bytes=64), reuse.tile([P, S], U32, name="v1", offset=16384, align_bytes=64)]
         v_s = keep.tile([P, S], U8, name="v_s", align_bytes=64)
         sig_late = keep.tile([P, 4, 1024], F32, name="sig_late")
         sig2 = {(1, g): sig_late[:, g] for g in range(4)}
@@ -69,7 +69,8 @@ def tile_list_bond_softplus_store_kernel(
         ident = keep.tile([P, P], F32, name="ident")
         h_q = {(r, half): keep.tile([P, 4 * JC], U32, name=f"h_q{r}{half}", align_bytes=64) for r in range(2) for half in range(2)}
         h_s = {(r, half): keep.tile([P, 4 * JC], U8, name=f"h_s{r}{half}", align_bytes=64) for r in range(2) for half in range(2)}
-        win = [keep.tile([P, T2], F32, name=f"win{q}") for q in range(4)]
+        win = [keep.tile([P, T2], F32, name=f"win{q}") for q in range(2)]
+        win = win + [reuse.tile([P, T2], F32, name=f"win{q}", offset=8192 * q, align_bytes=64) for q in range(2, 4)]
 
         def load_w(k):
             for a in range(2):
@@ -219,7 +220,7 @@ def tile_list_bond_softplus_store_kernel(
             name = "y" + "".join(f"{q}{lo}" for q, lo, hi in parts)
             width = sum(hi - lo for q, lo, hi in parts)
             bank = psum.tile([P, 512], F32, name=name, tag=f"bank{slot}")
-            wd = 512 if parts[0][2] - parts[0][1] == 512 else JC
+            wd = parts[0][2] - parts[0][1]
             at = 0
             for q, lo, hi in parts:
                 for c0 in range(lo, hi, wd):
@@ -299,7 +300,7 @@ def tile_list_bond_softplus_store_kernel(
         eps_c = keep.tile([P, 4], F32, name="eps_c")
         nc.scalar.activation(eps_c[:], sig_late[:, :, 1023], ACT.Copy, scale=0.0, bias=EPS)
         for q in range(4):
-            (nc.gpsimd if q < 2 else nc.vector).memset(win[q][:].bitcast(I32), 0)
+            (nc.vector if q < 2 else nc.gpsimd).memset(win[q][:].bitcast(I32), 0)
 
         finish_on_vector(0, 0, 2)
         finish_on_vector(0, 1, 3)

@@ -325,9 +325,9 @@ def tile_list_bond_softplus_store_kernel(
         finish_on_scalar(1, 2, [5, 1])
         second_product([(3, 0, 512)], 1)
         finish_on_scalar(0, 3, [7, 2])
-        second_product([(0, 512, 768)], 2)
+        second_product([(0, 512, 768), (1, 512, 768)], 2)
         finish_on_scalar(1, 3, [3, 4])
-        second_product([(1, 512, 768)], 4)
+        second_product([(2, 512, 768)], 4)
         second_product([(0, 768, 1024), (1, 768, 1024)], 0)
-        second_product([(2, 512, 1024)], 6)
+        second_product([(2, 768, 1024)], 6)
         second_product([(3, 512, 1024)], 5)

import math
from contextlib import ExitStack

import concourse.mybir as mybir
from concourse.masks import make_identity

K, H, N, T, S, T2 = 1024, 1024, 512, 2048, 1024, 2048
FLOPS = 2 * K * H * S + 2 * H * N * S

F32 = mybir.dt.float32
BF16 = mybir.dt.bfloat16
I32 = mybir.dt.int32
U32 = mybir.dt.uint32
U16 = mybir.dt.uint16
U8 = mybir.dt.uint8
FP8X4 = mybir.dt.float8_e4m3fn_x4
FP4X4 = mybir.dt.float4_e2m1fn_x4
ALU = mybir.AluOpType
ACT = mybir.ActivationFunctionType

P = 128
JC = 128
NJC = S // JC
EPS = 2.0**-60
LN2 = math.log(2.0)
FLOOR = -20.0


def tile_list_bond_softplus_store_kernel(
    tc, tab_words, tab_scales, offs, w1, gain, w4_words, w4_scales, wgo, offs2, out
):
    nc = tc.nc
    with ExitStack() as ctx:
        keep = ctx.enter_context(tc.tile_pool(name="keep", bufs=1))
        reuse = ctx.enter_context(tc.tile_pool(name="reuse", bufs=1))
        psum = ctx.enter_context(tc.psum_pool(name="psum", bufs=1))

        offs_t = keep.tile([P, S // 16], U16, name="offs_t")
        offs2_t = keep.tile([P, S // 16], U16, name="offs2_t")
        tab_sc = keep.tile([P, T], U8, name="tab_sc", align_bytes=64)
        w4_sc = keep.tile([P, 2, N], U8, name="w4_sc", align_bytes=64)
        tab_w = [keep.tile([P, T], I32, name=f"tab_w{a}", align_bytes=64) for a in range(2)]
        w_raw = {(a, k): keep.tile([P, 4, 256], F32, name=f"w_raw{a}{k}") for k in range(2) for a in range(2)}
        for k in range(2, 4):
            for a in range(2):
                w_raw[a, k] = reuse.tile([P, 4, 256], F32, name=f"w_raw{a}{k}", offset=4096 * (2 * k + a - 4), align_bytes=64)
        w_bf = [reuse.tile([P, 2048], BF16, name="w_bf0", offset=16384, align_bytes=64)]
        w_bf = w_bf + [keep.tile([P, 2048], BF16, name=f"w_bf{k}", align_bytes=64) for k in range(1, 4)]
        w_q = [reuse.tile([P, 512], U32, name=f"w_q{k}", offset=24576 + 2048 * k, align_bytes=64) for k in range(4)]
        w_s = [keep.tile([P, 512], U8, name=f"w_s{k}", align_bytes=64) for k in range(4)]
        w4_t = keep.tile([P, 2, 2 * N], U8, name="w4_t", align_bytes=64)
        wgo_t = keep.tile([P, S], F32, name="wgo_t")
        gain_t = keep.tile([P, 2, 4], F32, name="gain_t")
        ngain = keep.tile([P, 2, 4], F32, name="ngain")
        v_w = [reuse.tile([P, S], U32, name="v0", offset=20480, align_bytes=64), reuse.tile([P, S], U32, name="v1", offset=16384, align_bytes=64)]
        v_s = keep.tile([P, S], U8, name="v_s", align_bytes=64)
        sig_late = keep.tile([P, 4, 1024], F32, name="sig_late")
        sig2 = {(1, g): sig_late[:, g] for g in range(4)}
        for g in range(4):
            sig2[0, g] = keep.tile([P, 1024], F32, name=f"sig0{g}")[:]
        nega2 = {(r, g): keep.tile([P, 1024], F32, name=f"nega{r}{g}")[:] for r in range(2) for g in range(2)}
        for r in range(2):
            for g in range(2, 4):
                nega2[r, g] = reuse.tile([P, 1024], F32, name=f"nega{r}{g}", offset=4096 * (2 * r + g - 2), align_bytes=64)[:]
        minus = keep.tile([P, 1], F32, name="minus")
        rc = [(r, c) for r in range(2) for c in range(NJC)]
        sig = {(r, c): sig2[r, c // 2][:, 512 * (c % 2) : 512 * (c % 2 + 1)] for r, c in rc}
        nega = {(r, c): nega2[r, c // 2][:, 512 * (c % 2) : 512 * (c % 2 + 1)] for r, c in rc}
        ident = keep.tile([P, P], F32, name="ident")
        h_q = {(r, half): keep.tile([P, 4 * JC], U32, name=f"h_q{r}{half}", align_bytes=64) for r in range(2) for half in range(2)}
        h_s = {(r, half): keep.tile([P, 4 * JC], U8, name=f"h_s{r}{half}", align_bytes=64) for r in range(2) for half in range(2)}
        win = [keep.tile([P, T2], F32, name=f"win{q}") for q in range(2)]
        win = win + [reuse.tile([P, T2], F32, name=f"win{q}", offset=8192 * q, align_bytes=64) for q in range(2, 4)]

        def load_w(k):
            for a in range(2):
                nc.sync.dma_start(
                    out=w_raw[a, k][:],
                    in_=w1[512 * a : 512 * a + 512, 256 * k : 256 * k + 256].rearrange("(p j) c -> p j c", j=4),
                )

        def load_tab(a):
            nc.sync.dma_start(out=tab_w[a][:], in_=tab_words[a].rearrange("p t i -> p (t i)").bitcast(I32))

        nc.gpsimd.memset(tab_sc[:].bitcast(I32), 0)
        nc.sync.dma_start(offs_t[:], offs)
        nc.sync.dma_start(offs2_t[:], offs2)
        load_tab(0)
        for qd in range(4):
            nc.sync.dma_start(
                out=tab_sc[32 * qd : 32 * qd + 8, :].bitcast(I32),
                in_=tab_scales[:, 4 * qd : 4 * qd + 4, :].bitcast(I32),
            )
        load_w(0)
        load_tab(1)
        for k in range(1, 4):
            load_w(k)
        nc.sync.dma_start(out=gain_t[:], in_=gain.rearrange("(a p t) -> p a t", a=2, t=4))
        nc.vector.memset(w4_sc[:].rearrange("p a n -> p (a n)").bitcast(I32), 0)
        for qd in range(4):
            nc.sync.dma_start(
                out=w4_sc[32 * qd : 32 * qd + 4, :, :].bitcast(I32),
                in_=w4_scales[:, 4 * qd : 4 * qd + 4, :].rearrange("a q n -> q a n").bitcast(I32),
            )
        nc.sync.dma_start(out=w4_t[:].bitcast(I32), in_=w4_words.rearrange("a p n -> p a n").bitcast(I32))
        nc.sync.dma_start(out=wgo_t[:], in_=wgo)

        def gather(a, lo, hi):
            nc.vector.tensor_copy(v_w[a][:, 256 * lo : 256 * hi], tab_w[a][:].bitcast(U32).indirect(offs_t[:, 16 * lo : 16 * hi]))

        def gather_scales(lo, hi):
            nc.vector.tensor_copy(v_s[:, 256 * lo : 256 * hi], tab_sc[:].indirect(offs_t[:, 16 * lo : 16 * hi]))

        def cast(a, k, copy):
            copy(
                w_bf[k][:, 1024 * a : 1024 * a + 1024].rearrange("p (m i j) -> p m j i", i=4, j=4),
                w_raw[a, k][:].rearrange("p j (m i) -> p m j i", i=4),
            )

        def quantise_w(k, lo, hi):
            cols = slice(256 * lo, 256 * hi)
            nc.vector.quantize_mx(out=w_q[k][:, cols].bitcast(FP8X4), scales=w_s[k][:, cols], in_=w_bf[k][:, 1024 * lo : 1024 * hi])

        banks = {}

        def product(k, g, slot):
            banks[k, g] = psum.tile([P, 2, 256], F32, name=f"a{k}{g}", tag=f"bank{slot}")
            for a in range(2):
                for i in range(2):
                    cols = slice(JC * (2 * g + i), JC * (2 * g + i + 1))
                    nc.tensor.matmul_mx(
                        out=banks[k, g][:, i, :],
                        lhsT=v_w[a][:, cols].bitcast(FP8X4),
                        lhsT_scale=v_s[4 * a : 128, cols],
                        rhs=w_q[k][:, 256 * a : 256 * a + 256].bitcast(FP8X4),
                        rhs_scale=w_s[k][:, 256 * a : 256 * a + 256],
                        start=(a == 0 and i == 0),
                        stop=(a == 1 and i == 1),
                    )

        def from_bank(k, g):
            return banks[k, g][:].rearrange("p i (m t) -> p i t m", t=4)

        def share(pair, k):
            return pair.rearrange("p (i t m) -> p i t m", i=2, t=4)[:, :, :, 64 * (k % 2) : 64 * (k % 2) + 64]

        def sigmoid_from_bank(k, g):
            nc.scalar.activation(share(sig2[k // 2, g], k), from_bank(k, g), ACT.Sigmoid)

        def copy_on_scalar(k, g):
            nc.scalar.activation(share(nega2[k // 2, g], k), from_bank(k, g), ACT.Copy, scale=-1.0)

        def copy_on_vector(k, g, factor):
            nc.vector.tensor_scalar(share(nega2[k // 2, g], k), from_bank(k, g), factor, None, ALU.mult)

        def floored_copy_then_sigmoid(k, g):
            dst = share(nega2[k // 2, g], k)
            nc.vector.tensor_scalar(dst, from_bank(k, g), FLOOR, -1.0, ALU.max, ALU.mult)
            nc.scalar.activation(share(sig2[k // 2, g], k), dst, ACT.Sigmoid, scale=-1.0)

        def turn(dst, src, t, start, stop):
            nc.tensor.matmul(dst, src[:, 128 * t : 128 * t + 128], ident[:], start=start, stop=stop, is_transpose=True)

        def log_of(x):
            nc.scalar.activation(x, x, ACT.Ln, bias=eps_c[:, 0:1], scale=2.0)

        def second_product(parts, slot):
            place(*multiply(parts, slot))

        h_bf = {}
        ys = []

        def h_tile(r, g):
            h_bf[r, g] = keep.tile([P, 1024], BF16, name=f"h_bf{r}{g}", align_bytes=64)
            return h_bf[r, g]

        def quantise_h(r, g):
            cols = slice(2 * JC * (g % 2), 2 * JC * (g % 2 + 1))
            nc.vector.quantize_mx(
                out=h_q[r, g // 2][:, cols].bitcast(FP8X4), scales=h_s[r, g // 2][:, cols], in_=h_bf[r, g][:, 0:1024]
            )

        def finish_on_vector(r, c, slot):
            i = c % 2
            dst = h_tile(r, c // 2) if i == 0 else h_bf[r, c // 2]
            u = psum.tile([P, 4, JC], F32, name=f"u{r}{c}", tag=f"bank{slot}")
            for t in range(4):
                turn(u[:, t, :], nega[r, c], t, t == 0, False)
            log_of(sig[r, c])
            for t in range(4):
                turn(u[:, t, :], sig[r, c], t, False, t == 3)
            nc.vector.scalar_tensor_tensor(
                dst[:, 512 * i : 512 * i + 512].rearrange("p (j t) -> p j t", t=4),
                u[:].rearrange("p t j -> p j t"),
                LN2,
                ngain[:, r].unsqueeze(1).to_broadcast([P, JC, 4]),
                ALU.min,
                ALU.mult,
            )

        def finish_on_scalar(r, g, slots):
            dst = h_tile(r, g)
            u = [psum.tile([P, 2, 2 * JC], F32, name=f"u{r}{g}{b}", tag=f"bank{slots[b]}") for b in range(2)]
            for i in range(2):
                for t in range(4):
                    turn(u[t // 2][:, t % 2, JC * i : JC * (i + 1)], nega[r, 2 * g + i], t, i == 0 and t % 2 == 0, False)
            for i in range(2):
                for t in range(4):
                    turn(u[t // 2][:, t % 2, JC * i : JC * (i + 1)], sig[r, 2 * g + i], t, False, i == 1 and t % 2 == 1)
            by_t = keep.tile([P, 4, 2 * JC], BF16, name=f"by_t{r}{g}")
            for t in range(4):
                nc.scalar.activation(by_t[:, t, :], u[t // 2][:, t % 2, :], ACT.Copy, scale=ngain[:, r, t : t + 1])
            nc.scalar.copy(
                dst[:, 0:1024].rearrange("p (c i t) -> p c t i", i=4, t=4),
                by_t[:].rearrange("p t (c i) -> p c t i", i=4),
            )
            quantise_h(r, g)

        def multiply(parts, slot):
            name = "y" + "".join(f"{q}{lo}" for q, lo, hi in parts)
            width = sum(hi - lo for q, lo, hi in parts)
            bank = psum.tile([P, 512], F32, name=name, tag=f"bank{slot}")
            wd = parts[0][2] - parts[0][1]
            at = 0
            for q, lo, hi in parts:
                for c0 in range(lo, hi, wd):
                    cols = slice(c0 % 512, c0 % 512 + wd)
                    for r in range(2):
                        nc.tensor.matmul_mx(
                            out=bank[:, at : at + wd],
                            lhsT=w4_t[:, r, 256 * q : 256 * q + 256].bitcast(FP4X4),
                            lhsT_scale=w4_sc[:, r, 128 * q : 128 * q + 128],
                            rhs=h_q[r, lo // 512][:, cols].bitcast(FP8X4),
                            rhs_scale=h_s[r, lo // 512][:, cols],
                            start=(r == 0),
                            stop=(r == 1),
                        )
                    at += wd
            return parts, bank, name, width

        def place(parts, bank, name, width):
            y = keep.tile([P, width], F32, name="s" + name)
            nc.scalar.copy(y[:], bank[:, 0:width])
            ys.append(y)
            at = 0
            for q, lo, hi in parts:
                nc.vector.tensor_tensor(
                    win[q][:].indirect(offs2_t[:, lo // 16 : hi // 16]), y[:, at : at + hi - lo], wgo_t[:, lo:hi], ALU.mult
                )
                at += hi - lo
                if hi == S:
                    nc.sync.dma_start(out=out[128 * q : 128 * q + 128, :], in_=win[q][:])

        make_identity(nc, ident[:])
        gather(0, 0, 4)
        gather_scales(0, 4)
        cast(0, 0, nc.scalar.copy)
        cast(1, 0, nc.scalar.copy)
        quantise_w(0, 0, 2)
        gather(1, 0, 1)
        gather(1, 1, 2)
        cast(0, 1, nc.vector.tensor_copy)
        cast(1, 1, nc.vector.tensor_copy)
        quantise_w(1, 0, 2)
        gather(1, 2, 4)
        for k in range(2, 4):
            cast(0, k, nc.scalar.copy)
            if k == 3:
                quantise_w(k, 0, 1)
            cast(1, k, nc.vector.tensor_copy)
            quantise_w(k, k - 2, 2)

        for g in range(2):
            product(0, g, g)
            sigmoid_from_bank(0, g)
            if g == 0:
                copy_on_scalar(0, g)
            else:
                copy_on_vector(0, g, -1.0)
        for g in range(2, 4):
            product(0, g, g)
            floored_copy_then_sigmoid(0, g)
        for g in range(2):
            product(1, g, 4 + g)
            sigmoid_from_bank(1, g)
        for g in range(2, 4):
            product(1, g, 4 + g)
            floored_copy_then_sigmoid(1, g)
        for k, slots in ((2, [0, 1, 2, 3]), (3, [6, 7, 2, 3])):
            for g in range(2):
                product(k, g + 2, slots[g + 2])
                product(k, g, slots[g])
                sigmoid_from_bank(k, g)
                floored_copy_then_sigmoid(k, g + 2)
        nc.gpsimd.tensor_scalar(ngain[:], gain_t[:], -1.0, 0.0, ALU.mult, ALU.add)
        nc.gpsimd.tensor_scalar(minus[:], nega2[1, 3][:, 0:1], 0.0, -1.0, ALU.mult, ALU.add)
        for g in range(2):
            for k in range(1, 4):
                copy_on_vector(k, g, minus[:, 0:1])
        eps_c = keep.tile([P, 4], F32, name="eps_c")
        nc.scalar.activation(eps_c[:], sig_late[:, :, 1023], ACT.Copy, scale=0.0, bias=EPS)
        for q in range(4):
            (nc.vector if q < 2 else nc.gpsimd).memset(win[q][:].bitcast(I32), 0)

        finish_on_vector(0, 0, 2)
        finish_on_vector(0, 1, 3)
        finish_on_vector(1, 0, 4)
        finish_on_vector(1, 1, 0)
        quantise_h(0, 0)
        quantise_h(1, 0)
        first = multiply([(0, 0, 256), (1, 0, 256)], 2)
        finish_on_vector(0, 2, 6)
        finish_on_vector(0, 3, 5)
        finish_on_vector(1, 2, 1)
        finish_on_vector(1, 3, 7)
        quantise_h(0, 1)
        quantise_h(1, 1)
        place(*first)
        second_product([(0, 256, 512), (1, 256, 512)], 3)
        second_product([(2, 0, 512)], 4)
        for g in range(2, 4):
            log_of(sig2[0, g])
            log_of(sig2[1, g])
        finish_on_scalar(0, 2, [0, 6])
        finish_on_scalar(1, 2, [5, 1])
        second_product([(3, 0, 512)], 1)
        finish_on_scalar(0, 3, [7, 2])
        second_product([(0, 512, 768), (1, 512, 768)], 2)
        finish_on_scalar(1, 3, [3, 4])
        second_product([(2, 512, 768)], 4)
        second_product([(0, 768, 1024), (1, 768, 1024)], 0)
        second_product([(2, 768, 1024)], 6)
        second_product([(3, 512, 1024)], 5)
